import numpy as np
import ml_dtypes


def mxq(x, axis, fmt="e4m3"):
    dtype, down = {"e4m3": (ml_dtypes.float8_e4m3fn, 7), "e5m2": (ml_dtypes.float8_e5m2, 14)}[fmt]
    v = np.moveaxis(np.asarray(x, np.float32).astype(ml_dtypes.bfloat16).astype(np.float64), axis, -1)
    blocks = v.reshape(v.shape[:-1] + (-1, 32))
    amax = np.abs(blocks).max(-1, keepdims=True)
    byte = np.maximum(np.where(amax > 0, np.frexp(amax)[1] - 1 + 127, 0) - down, 1)
    scale = np.exp2(byte - 127.0)
    codes = (blocks / scale).astype(np.float32).astype(dtype).astype(np.float64)
    return np.moveaxis((codes * scale).reshape(v.shape), -1, axis)


WIDE = False


def mx_kscale(k):
    if not WIDE:
        return np.ones(k)
    levels = np.array([10, -10, 5, -5, 0])
    if k % 512:
        return np.exp2(np.random.permutation(np.resize(levels, k // 32))).repeat(32)
    a = np.empty((k // 512, 16))
    for p in range(k // 512):
        a[p, :8] = np.random.permutation(np.resize(levels, 8))
        for g in range(8):
            far = levels[np.abs(levels - a[p, g]) >= 10]
            a[p, g + 8] = far[np.random.randint(len(far))]
    return np.exp2(a.ravel()).repeat(32)


def f64(x):
    return np.asarray(x).astype(np.float64)


def striped(idx):
    return np.tile(np.asarray(idx).reshape(-1, 16).T, (8, 1)).astype(np.uint16)


def unstriped(offs):
    return offs[:16].T.reshape(-1).astype(np.int64)


E2M1 = np.array([0.0, 0.5, 1.0, 1.5, 2.0, 3.0, 4.0, 6.0, -0.0, -0.5, -1.0, -1.5, -2.0, -3.0, -4.0, -6.0])


def pack_weight(w, fmt):
    k, n = w.shape
    w = f64(np.asarray(w, np.float32).astype(ml_dtypes.bfloat16)).reshape(k // 32, 32, n)
    amax = np.abs(w).max(1)
    if fmt == "e4m3":
        byte = np.frexp(amax)[1] - 1 + 127 - 7
    else:
        mant, ex = np.frexp(amax / 6.0)
        byte = np.where(mant > 0.5, ex, ex - 1) + 127
    byte = np.clip(np.where(amax > 0, byte, 1), 1, 254)
    scaled = (w * np.exp2(127.0 - byte)[:, None, :]).reshape(k, n).astype(np.float32)
    by_word = np.ascontiguousarray(scaled.reshape(k // 512, 128, 4, n).transpose(0, 1, 3, 2))
    if fmt == "e4m3":
        words = by_word.astype(ml_dtypes.float8_e4m3fn).view(np.uint8)
    else:
        c = by_word.astype(ml_dtypes.float4_e2m1fn).view(np.uint8) & 0xF
        words = (c[..., 0::2] | (c[..., 1::2] << 4)).reshape(k // 512, 128, 2 * n)
    return np.ascontiguousarray(words), np.ascontiguousarray(byte.astype(np.uint8).reshape(k // 512, 16, n))


def unpack_weight(words, scales, fmt):
    g, _, n = scales.shape
    words = np.ascontiguousarray(words).reshape(g, 128, n, -1)
    if fmt == "e4m3":
        vals = words.view(ml_dtypes.float8_e4m3fn).astype(np.float64)
    else:
        nib = np.empty((g, 128, n, 4), np.uint8)
        nib[..., 0::2] = words & 0xF
        nib[..., 1::2] = words >> 4
        vals = E2M1[nib]
    vals = vals * np.repeat(np.exp2(scales.astype(np.float64) - 127.0), 8, axis=1)[..., None]
    return vals.transpose(0, 1, 3, 2).reshape(g * 512, n)


def bf(x):
    return np.asarray(x, np.float32).astype(ml_dtypes.bfloat16)


def planes(Y):
    r, m = Y.shape
    b = f64(bf(Y)).reshape(r // 32, 32, m)
    amax = np.abs(b).max(1)
    byte = np.clip(np.where(amax > 0, np.frexp(amax)[1] - 1 + 127 - 7, 1), 1, 254)
    codes = (b * np.exp2(127.0 - byte)[:, None, :]).reshape(r, m).astype(np.float32).astype(ml_dtypes.float8_e4m3fn).view(np.uint8)
    words = codes.reshape(r // 512, 128, 4, m).transpose(0, 1, 3, 2)
    return np.ascontiguousarray(words), np.ascontiguousarray(byte.astype(np.uint8).reshape(r // 512, 16, m))


D, I, Q, E, U = 512, 512, 256, 512, 512


def setup_inputs():
    n = np.random.standard_normal
    idx = np.random.randint(0, U, I)
    idx2 = np.random.randint(0, U, I)
    idx3 = np.random.randint(0, U, I)
    fd = mx_kscale(D)
    fi = mx_kscale(I)
    bap = pack_weight(n((D, U)) / fd[:, None], "e2m1")
    bbp = pack_weight(n((D, U)) * 0.6 / fd[:, None], "e4m3")
    bcp = pack_weight(n((D, U)) * 0.4 / fd[:, None], "e4m3")
    return {
        "query": (n((D, Q)) * 0.25 / np.sqrt(D) * fd[:, None]).astype(np.float32),
        "ba_words": bap[0],
        "ba_scales": bap[1],
        "bb_words": bbp[0],
        "bb_scales": bbp[1],
        "bc_words": bcp[0],
        "bc_scales": bcp[1],
        "size": (np.random.uniform(0.5, 2.0, (1, I)) * fi).astype(np.float32),
        "ca": (n((E, U))).astype(np.float32),
        "cb": (n((E, U)) * 0.6).astype(np.float32),
        "cc": (n((E, U)) * 0.4).astype(np.float32),
        "vsc": (np.random.uniform(0.5, 2.0, (I, 1)) / fi[:, None]).astype(np.float32),
        "offs": striped(idx),
        "offs2": striped(idx2),
        "offs3": striped(idx3),
    }


def reference(query, ba_words, ba_scales, bb_words, bb_scales, bc_words, bc_scales, size, ca, cb, cc, vsc, offs, offs2, offs3):
    idx = unstriped(offs)
    idx2 = unstriped(offs2)
    idx3 = unstriped(offs3)
    bau = unpack_weight(ba_words, ba_scales, "e2m1")
    bbu = unpack_weight(bb_words, bb_scales, "e4m3")
    bcu = unpack_weight(bc_words, bc_scales, "e4m3")
    queryq = mxq(f64(query), 0, "e4m3")
    baidxg = bau[:, idx]
    bbidx2g = bbu[:, idx2]
    bcidx3g = bcu[:, idx3]
    a = queryq.T @ baidxg + queryq.T @ bbidx2g + queryq.T @ bcidx3g
    p = np.exp(a - np.max(a, axis=1, keepdims=True))
    w = p * f64(size) / np.sum(p, axis=1, keepdims=True)
    wt = w.T
    va = f64(ca)[:, idx].T
    vb = f64(cb)[:, idx2].T
    vc = f64(cc)[:, idx3].T
    vv = (va + vb + vc) * f64(vsc)
    vvq = mxq(vv, 0, "e4m3")
    wtq = mxq(wt, 0, "e4m3")
    o = vvq.T @ wtq
    words, scales = planes(o)
    return o, words, scales

@@ -1,0 +1,200 @@
+from contextlib import ExitStack
+
+import concourse.mybir as mybir
+from concourse.masks import make_identity
+
+D, I, Q, E, U = 512, 512, 256, 512, 512
+FLOPS = 2 * (3 * D * Q * I + I * E * Q)
+
+F32 = mybir.dt.float32
+BF16 = mybir.dt.bfloat16
+I32 = mybir.dt.int32
+U32 = mybir.dt.uint32
+U16 = mybir.dt.uint16
+U8 = mybir.dt.uint8
+FP8X4 = mybir.dt.float8_e4m3fn_x4
+FP4X4 = mybir.dt.float4_e2m1fn_x4
+ACT = mybir.ActivationFunctionType
+ALU = mybir.AluOpType
+AXIS = mybir.AxisListType
+
+P = 128
+PACK = 4
+WIN = 704
+WIN16 = 1024
+SPARE = WIN - U
+HALVES = Q // P
+
+
+def tile_attend_additivekeys_pl_kernel(tc, query, ba_words, ba_scales, bb_words, bb_scales, bc_words, bc_scales,
+                                        size, ca, cb, cc, vsc, offs, offs2, offs3, out_0, out_1, out_2):
+    nc = tc.nc
+    with ExitStack() as ctx:
+        keep = ctx.enter_context(tc.tile_pool(name="keep", bufs=1))
+        psum = ctx.enter_context(tc.psum_pool(name="psum", bufs=1))
+
+        lists = [keep.tile([P, I // 16], U16, name=f"list{b}") for b in range(3)]
+        key_tab = [keep.tile([P, 2 * WIN16], U8, name="key_tab0"),
+                   keep.tile([P, WIN], I32, name="key_tab1"),
+                   keep.tile([P, WIN], I32, name="key_tab2")]
+        scale_tab = [keep.tile([P, WIN], U8, name=f"scale_tab{b}", tag=f"scale_tab{b}") for b in range(3)]
+        val_tab = [[keep.tile([P, U + WIN], F32, name=f"val_tab{b}_{u}") for u in range(2)] for b in range(3)]
+        ident = keep.tile([P, P], F32, name="ident")
+
+        for b in range(3):
+            nc.vector.memset(scale_tab[b][:].bitcast(I32), 0)
+        nc.vector.memset(key_tab[0][:, 2 * U:].bitcast(I32), 0)
+        for b in (1, 2):
+            nc.vector.memset(key_tab[b][:, U:], 0)
+        make_identity(nc, ident[:])
+        for u in range(2):
+            for b in range(3):
+                nc.gpsimd.memset(val_tab[b][u][:, 2 * U:], 0.0)
+
+        nc.sync.dma_start(lists[0][:], offs)
+        nc.scalar.dma_start(key_tab[0][:, :2 * U].bitcast(I32), ba_words[0].bitcast(I32))
+        nc.sync.dma_start(lists[1][:], offs2)
+        nc.sync.dma_start(key_tab[1][:, :U], bb_words[0].rearrange("p n t -> p (n t)").bitcast(I32))
+        nc.sync.dma_start(lists[2][:], offs3)
+        nc.sync.dma_start(key_tab[2][:, :U], bc_words[0].rearrange("p n t -> p (n t)").bitcast(I32))
+        q_raw = keep.tile([P, PACK, Q], F32, name="q_raw")
+        nc.sync.dma_start(q_raw[:], query.rearrange("(p t) q -> p t q", t=PACK))
+        for b, scales in enumerate((ba_scales, bb_scales, bc_scales)):
+            for quad in range(4):
+                nc.sync.dma_start(scale_tab[b][32 * quad:32 * quad + 4, :U].bitcast(I32),
+                                  scales[0, 4 * quad:4 * quad + 4, :].bitcast(I32))
+        size_t = keep.tile([P, PACK], F32, name="size_t")
+        vsc_t = keep.tile([P, PACK], F32, name="vsc_t")
+        for u in range(2):
+            for b, table in enumerate((ca, cb, cc)):
+                rows = table.rearrange("(p t) u -> p (t u)", t=PACK)
+                nc.sync.dma_start(val_tab[b][u][:, :2 * U], rows[:, 2 * U * u:2 * U * (u + 1)])
+            if u == 0:
+                nc.sync.dma_start(vsc_t[:], vsc.rearrange("(p t) o -> p (t o)", t=PACK))
+                nc.sync.dma_start(size_t[:], size.rearrange("o (p t) -> (o p) t", t=PACK))
+
+        q_bf = keep.tile([P, Q, PACK], BF16, name="q_bf", align_bytes=64)
+        nc.scalar.copy(q_bf[:].rearrange("p (c i) t -> p c t i", i=4),
+                       q_raw[:].rearrange("p t (c i) -> p c t i", i=4))
+        q_codes = keep.tile([P, Q], U32, name="q_codes", align_bytes=64)
+        q_scales = keep.tile([P, Q], U8, name="q_scales", align_bytes=64)
+        nc.vector.quantize_mx(out=q_codes[:].bitcast(FP8X4), scales=q_scales[:],
+                              in_=q_bf[:].rearrange("p q t -> p (q t)"))
+
+        key = [keep.tile([P, 2 * I], U8, name="key0", align_bytes=64),
+               keep.tile([P, I], U32, name="key1", align_bytes=64),
+               keep.tile([P, I], U32, name="key2", align_bytes=64)]
+        key_scale = [keep.tile([P, I], U8, name=f"key_scale{b}", align_bytes=64) for b in range(3)]
+        nc.vector.tensor_copy(key[0][:].bitcast(U16), key_tab[0][:].bitcast(U16).indirect(lists[0][:]))
+        for b in (1, 2):
+            nc.vector.tensor_copy(key[b][:], key_tab[b][:].bitcast(U32).indirect(lists[b][:]))
+        score = [psum.tile([P, I], F32, name=f"score{h}") for h in range(HALVES)]
+        for b in range(3):
+            nc.vector.tensor_copy(key_scale[b][:], scale_tab[b][:].indirect(lists[b][:]))
+            for h in range(HALVES):
+                cols = slice(P * h, P * (h + 1))
+                nc.tensor.matmul_mx(out=score[h][:], lhsT=q_codes[:, cols].bitcast(FP8X4), lhsT_scale=q_scales[:, cols],
+                                    rhs=key[b][:].bitcast(FP4X4 if b == 0 else FP8X4), rhs_scale=key_scale[b][:],
+                                    start=(b == 0), stop=(b == 2))
+
+        neg_max = keep.tile([P, HALVES], F32, name="neg_max")
+        row_sum = keep.tile([P, HALVES], F32, name="row_sum")
+        inv_sum = keep.tile([P, HALVES], F32, name="inv_sum")
+        prob = [keep.tile([P, PACK, P], F32, name=f"prob{h}") for h in range(HALVES)]
+        for h in range(HALVES):
+            nc.vector.tensor_reduce(neg_max[:, h:h + 1], score[h][:], AXIS.X, ALU.max, negate=True)
+            nc.scalar.activation(prob[h][:], score[h][:].rearrange("p (s t) -> p t s", t=PACK), ACT.Exp,
+                                 bias=neg_max[:, h:h + 1], accum_out=row_sum[:, h:h + 1])
+        nc.vector.reciprocal(inv_sum[:], row_sum[:])
+        w_planes = keep.tile([P, PACK, Q], BF16, name="w_planes")
+        early_bf = keep.tile([P, Q + 2 * P, PACK], BF16, name="early_bf", tag="early", align_bytes=64)
+        early_codes = keep.tile([P, Q + 2 * P], U32, name="early_codes", align_bytes=64)
+        early_scales = keep.tile([P, Q + 2 * P], U8, name="early_scales", align_bytes=64)
+        w_turned = [psum.tile([P, 2, Q], F32, name=f"w_turned{u}", tag=f"turn{u + 1}") for u in range(2)]
+        for h in range(HALVES):
+            normed = keep.tile([P, PACK, P], F32, name=f"normed{h}")
+            nc.scalar.activation(normed[:], prob[h][:], ACT.Copy, scale=inv_sum[:, h:h + 1])
+            for t in range(PACK):
+                nc.tensor.transpose(w_turned[t // 2][:, t % 2, P * h:P * (h + 1)], normed[:, t, :], ident[:])
+        for t in range(PACK):
+            nc.scalar.activation(w_planes[:, t, :], w_turned[t // 2][:, t % 2, :], ACT.Copy, scale=size_t[:, t:t + 1])
+        nc.scalar.copy(early_bf[:, :Q, :].rearrange("p (c i) t -> p c t i", i=4),
+                       w_planes[:].rearrange("p t (c i) -> p c t i", i=4))
+
+        acc = [psum.tile([P, PACK, P], F32, name=f"acc{h}") for h in range(HALVES)]
+        o_sb = keep.tile([P, PACK, Q], F32, name="o_sb")
+        o_rows = out_0.rearrange("(p t) q -> p t q", t=PACK)
+        o_bf = keep.tile([P, Q, PACK], BF16, name="o_bf", align_bytes=64)
+
+        def gather_and_turn(j, picked):
+            summed = psum.tile([P, PACK, P], F32, name=f"summed{j}", tag=f"turn{j % 3}")
+            for b in range(3):
+                window = val_tab[b][j // 2][:, U * (j % 2):U * (j % 2) + WIN]
+                nc.vector.tensor_copy(picked[b].bitcast(U32).rearrange("p t s -> p s t"),
+                                      window.bitcast(U32).indirect(lists[b][:]))
+                for t in range(PACK):
+                    nc.tensor.matmul(summed[:, t, :], lhsT=picked[b][:, t, :], rhs=ident[:], is_transpose=True,
+                                     start=(b == 0 and t == 0), stop=(b == 2 and t == PACK - 1))
+            return summed
+
+        def scale_on_scalar(j, summed, v_bf):
+            v_planes = keep.tile([P, PACK, P], BF16, name=f"v_planes{j}")
+            for t in range(PACK):
+                nc.scalar.activation(v_planes[:, t, :], summed[:, t, :], ACT.Copy, scale=vsc_t[:, t:t + 1])
+            nc.scalar.copy(v_bf.rearrange("p (c i) t -> p c t i", i=4),
+                           v_planes[:].rearrange("p t (c i) -> p c t i", i=4))
+
+        def product(j, v_codes, v_scales):
+            for h in range(HALVES):
+                cols = slice(P * h, P * (h + 1))
+                nc.tensor.matmul_mx(out=acc[h][:, j, :], lhsT=v_codes.bitcast(FP8X4), lhsT_scale=v_scales,
+                                    rhs=early_codes[:, cols].bitcast(FP8X4), rhs_scale=early_scales[:, cols],
+                                    start=True, stop=True)
+
+        def store(j0, j1):
+            for h in range(HALVES):
+                nc.scalar.copy(o_sb[:, j0:j1, P * h:P * (h + 1)], acc[h][:, j0:j1, :])
+            nc.sync.dma_start(o_rows[:, j0:j1, :], o_sb[:, j0:j1, :])
+
+        for j in range(2):
+            picked = [keep.tile([P, PACK, P], F32, name=f"picked{j}_{b}",
+                                tag="scale_tab2" if (j, b) == (0, 0) else f"picked{j}_{b}")[:] for b in range(3)]
+            summed = gather_and_turn(j, picked)
+            scale_on_scalar(j, summed, early_bf[:, Q + P * j:Q + P * (j + 1), :])
+        picked = [keep.tile([P, PACK, P], F32, name=f"picked2_{b}")[:] for b in range(3)]
+        summed2 = gather_and_turn(2, picked)
+        nc.vector.quantize_mx(out=early_codes[:].bitcast(FP8X4), scales=early_scales[:],
+                              in_=early_bf[:].rearrange("p m t -> p (m t)"))
+        for j in range(2):
+            cols = slice(Q + P * j, Q + P * (j + 1))
+            product(j, early_codes[:, cols], early_scales[:, cols])
+        store(0, 2)
+        late_bf = [keep.tile([P, P, PACK], BF16, name=f"late_bf{j}", align_bytes=64) for j in range(2)]
+        late_codes = [keep.tile([P, P], U32, name=f"late_codes{j}", align_bytes=64) for j in range(2)]
+        late_scales = [keep.tile([P, P], U8, name=f"late_scales{j}", align_bytes=64) for j in range(2)]
+        scale_on_scalar(2, summed2, late_bf[0][:])
+        picked = [keep.tile([P, PACK, P], F32, name=f"picked3_{b}", tag="early" if b == 2 else f"picked3_{b}",
+                            align_bytes=64)[:] for b in range(3)]
+        summed3 = gather_and_turn(3, picked)
+        nc.vector.quantize_mx(out=late_codes[0][:].bitcast(FP8X4), scales=late_scales[0][:],
+                              in_=late_bf[0][:].rearrange("p m t -> p (m t)"))
+        product(2, late_codes[0][:], late_scales[0][:])
+        store(2, 3)
+        nc.vector.tensor_tensor(late_bf[1][:], summed3[:].rearrange("p t m -> p m t"),
+                                vsc_t[:].unsqueeze(1).to_broadcast([P, P, PACK]), ALU.mult)
+        nc.vector.quantize_mx(out=late_codes[1][:].bitcast(FP8X4), scales=late_scales[1][:],
+                              in_=late_bf[1][:].rearrange("p m t -> p (m t)"))
+        product(3, late_codes[1][:], late_scales[1][:])
+        nc.vector.tensor_copy(o_bf[:, :P, :], acc[0][:].rearrange("p t q -> p q t"))
+        nc.scalar.copy(o_bf[:, P:, :], acc[1][:].rearrange("p t q -> p q t"))
+        store(3, 4)
+
+        o_codes = keep.tile([P, Q], U32, name="o_codes", align_bytes=64)
+        o_scales = keep.tile([P, Q], U8, name="o_scales", align_bytes=64)
+        nc.vector.quantize_mx(out=o_codes[:].bitcast(FP8X4), scales=o_scales[:],
+                              in_=o_bf[:].rearrange("p q t -> p (q t)"))
+        nc.sync.dma_start(out_1[0].rearrange("p c t -> p (c t)").bitcast(I32), o_codes[:].bitcast(I32))
+        for quad in range(4):
+            queue = nc.sync if quad % 2 == 0 else nc.scalar
+            queue.dma_start(out_2[0, 4 * quad:4 * quad + 4, :].bitcast(I32),
+                            o_scales[32 * quad:32 * quad + 4, :].bitcast(I32))

@@ -24,6 +24,7 @@ WIN = 704
 WIN16 = 1024
 SPARE = WIN - U
 HALVES = Q // P
+START = (0, U, U, 0)
 
 
 def tile_attend_additivekeys_pl_kernel(tc, query, ba_words, ba_scales, bb_words, bb_scales, bc_words, bc_scales,
@@ -59,19 +60,21 @@ def tile_attend_additivekeys_pl_kernel(tc, query, ba_words, ba_scales, bb_words,
         nc.sync.dma_start(key_tab[2][:, :U], bc_words[0].rearrange("p n t -> p (n t)").bitcast(I32))
         q_raw = keep.tile([P, PACK, Q], F32, name="q_raw")
         nc.sync.dma_start(q_raw[:], query.rearrange("(p t) q -> p t q", t=PACK))
+        val_rows = [table.rearrange("(p t) u -> p (t u)", t=PACK) for table in (ca, cb, cc)]
+        nc.sync.dma_start(val_tab[0][0][:, :2 * U], val_rows[0][:, :2 * U])
         for b, scales in enumerate((ba_scales, bb_scales, bc_scales)):
             for quad in range(4):
                 nc.sync.dma_start(scale_tab[b][32 * quad:32 * quad + 4, :U].bitcast(I32),
                                   scales[0, 4 * quad:4 * quad + 4, :].bitcast(I32))
         size_t = keep.tile([P, PACK], F32, name="size_t")
         vsc_t = keep.tile([P, PACK], F32, name="vsc_t")
-        for u in range(2):
-            for b, table in enumerate((ca, cb, cc)):
-                rows = table.rearrange("(p t) u -> p (t u)", t=PACK)
-                nc.sync.dma_start(val_tab[b][u][:, :2 * U], rows[:, 2 * U * u:2 * U * (u + 1)])
-            if u == 0:
-                nc.sync.dma_start(vsc_t[:], vsc.rearrange("(p t) o -> p (t o)", t=PACK))
-                nc.sync.dma_start(size_t[:], size.rearrange("o (p t) -> (o p) t", t=PACK))
+        for b in (1, 2):
+            nc.sync.dma_start(val_tab[b][0][:, :2 * U], val_rows[b][:, :2 * U])
+        nc.sync.dma_start(vsc_t[:], vsc.rearrange("(p t) o -> p (t o)", t=PACK))
+        nc.sync.dma_start(size_t[:], size.rearrange("o (p t) -> (o p) t", t=PACK))
+        for j in (2, 3):
+            for b in range(3):
+                nc.sync.dma_start(val_tab[b][1][:, START[j]:START[j] + U], val_rows[b][:, U * j:U * (j + 1)])
 
         q_bf = keep.tile([P, Q, PACK], BF16, name="q_bf", align_bytes=64)
         nc.scalar.copy(q_bf[:].rearrange("p (c i) t -> p c t i", i=4),
@@ -84,11 +87,11 @@ def tile_attend_additivekeys_pl_kernel(tc, query, ba_words, ba_scales, bb_words,
         key = [keep.tile([P, 2 * I], U8, name="key0", align_bytes=64),
                keep.tile([P, I], U32, name="key1", align_bytes=64),
                keep.tile([P, I], U32, name="key2", align_bytes=64)]
-        key_scale = [keep.tile([P, I], U8, name=f"key_scale{b}", align_bytes=64) for b in range(3)]
+        key_scale = [keep.tile([P, I], U8, name=f"key_scale{b}", tag=f"key_scale{b}", align_bytes=64) for b in range(3)]
         nc.vector.tensor_copy(key[0][:].bitcast(U16), key_tab[0][:].bitcast(U16).indirect(lists[0][:]))
         for b in (1, 2):
             nc.vector.tensor_copy(key[b][:], key_tab[b][:].bitcast(U32).indirect(lists[b][:]))
-        score = [psum.tile([P, I], F32, name=f"score{h}") for h in range(HALVES)]
+        score = [psum.tile([P, I], F32, name=f"score{h}", tag=f"score{h}") for h in range(HALVES)]
         for b in range(3):
             nc.vector.tensor_copy(key_scale[b][:], scale_tab[b][:].indirect(lists[b][:]))
             for h in range(HALVES):
@@ -98,7 +101,7 @@ def tile_attend_additivekeys_pl_kernel(tc, query, ba_words, ba_scales, bb_words,
                                     start=(b == 0), stop=(b == 2))
 
         neg_max = keep.tile([P, HALVES], F32, name="neg_max")
-        row_sum = keep.tile([P, HALVES], F32, name="row_sum")
+        row_sum = keep.tile([P, HALVES], F32, name="row_sum", tag="row_sum")
         inv_sum = keep.tile([P, HALVES], F32, name="inv_sum")
         prob = [keep.tile([P, PACK, P], F32, name=f"prob{h}") for h in range(HALVES)]
         for h in range(HALVES):
@@ -107,7 +110,7 @@ def tile_attend_additivekeys_pl_kernel(tc, query, ba_words, ba_scales, bb_words,
                                  bias=neg_max[:, h:h + 1], accum_out=row_sum[:, h:h + 1])
         nc.vector.reciprocal(inv_sum[:], row_sum[:])
         w_planes = keep.tile([P, PACK, Q], BF16, name="w_planes")
-        early_bf = keep.tile([P, Q + 2 * P, PACK], BF16, name="early_bf", tag="early", align_bytes=64)
+        early_bf = keep.tile([P, Q + 3 * P, PACK], BF16, name="early_bf", tag="early", align_bytes=64)
         early_codes = keep.tile([P, Q + 2 * P], U32, name="early_codes", align_bytes=64)
         early_scales = keep.tile([P, Q + 2 * P], U8, name="early_scales", align_bytes=64)
         w_turned = [psum.tile([P, 2, Q], F32, name=f"w_turned{u}", tag=f"turn{u + 1}") for u in range(2)]
@@ -121,7 +124,8 @@ def tile_attend_additivekeys_pl_kernel(tc, query, ba_words, ba_scales, bb_words,
         nc.scalar.copy(early_bf[:, :Q, :].rearrange("p (c i) t -> p c t i", i=4),
                        w_planes[:].rearrange("p t (c i) -> p c t i", i=4))
 
-        acc = [psum.tile([P, PACK, P], F32, name=f"acc{h}") for h in range(HALVES)]
+        acc = [[psum.tile([P, 2, P], F32, name=f"acc{u}_{h}", tag=f"score{h}" if u == 0 else f"acc{h}")
+                for h in range(HALVES)] for u in range(2)]
         o_sb = keep.tile([P, PACK, Q], F32, name="o_sb")
         o_rows = out_0.rearrange("(p t) q -> p t q", t=PACK)
         o_bf = keep.tile([P, Q, PACK], BF16, name="o_bf", align_bytes=64)
@@ -129,7 +133,7 @@ def tile_attend_additivekeys_pl_kernel(tc, query, ba_words, ba_scales, bb_words,
         def gather_and_turn(j, picked):
             summed = psum.tile([P, PACK, P], F32, name=f"summed{j}", tag=f"turn{j % 3}")
             for b in range(3):
-                window = val_tab[b][j // 2][:, U * (j % 2):U * (j % 2) + WIN]
+                window = val_tab[b][j // 2][:, START[j]:START[j] + WIN]
                 nc.vector.tensor_copy(picked[b].bitcast(U32).rearrange("p t s -> p s t"),
                                       window.bitcast(U32).indirect(lists[b][:]))
                 for t in range(PACK):
@@ -147,47 +151,58 @@ def tile_attend_additivekeys_pl_kernel(tc, query, ba_words, ba_scales, bb_words,
         def product(j, v_codes, v_scales):
             for h in range(HALVES):
                 cols = slice(P * h, P * (h + 1))
-                nc.tensor.matmul_mx(out=acc[h][:, j, :], lhsT=v_codes.bitcast(FP8X4), lhsT_scale=v_scales,
+                nc.tensor.matmul_mx(out=acc[j // 2][h][:, j % 2, :], lhsT=v_codes.bitcast(FP8X4), lhsT_scale=v_scales,
                                     rhs=early_codes[:, cols].bitcast(FP8X4), rhs_scale=early_scales[:, cols],
                                     start=True, stop=True)
 
-        def store(j0, j1):
-            for h in range(HALVES):
-                nc.scalar.copy(o_sb[:, j0:j1, P * h:P * (h + 1)], acc[h][:, j0:j1, :])
-            nc.sync.dma_start(o_rows[:, j0:j1, :], o_sb[:, j0:j1, :])
+        def unload(u, h):
+            nc.scalar.copy(o_sb[:, 2 * u:2 * u + 2, P * h:P * (h + 1)], acc[u][h][:])
 
-        for j in range(2):
-            picked = [keep.tile([P, PACK, P], F32, name=f"picked{j}_{b}",
-                                tag="scale_tab2" if (j, b) == (0, 0) else f"picked{j}_{b}")[:] for b in range(3)]
-            summed = gather_and_turn(j, picked)
+        def weave(u, h):
+            copy = nc.vector.tensor_copy if h == 0 else nc.scalar.copy
+            copy(o_bf[:, P * h:P * (h + 1), 2 * u:2 * u + 2], acc[u][h][:].rearrange("p j q -> p q j"))
+
+        def store(u):
+            queue = nc.sync if u == 0 else nc.scalar
+            queue.dma_start(o_rows[:, 2 * u:2 * u + 2, :], o_sb[:, 2 * u:2 * u + 2, :])
+
+        picked = {(0, 0): keep.tile([P, PACK, P], F32, name="picked00")[:],
+                  (1, 0): keep.tile([P, PACK, P], F32, name="picked10", tag="scale_tab2")[:],
+                  (0, 1): keep.tile([P, PACK, P], F32, name="picked01", tag="key_scale2", align_bytes=64)[:]}
+        rest = [(j, b) for j in range(PACK) for b in range(3) if (j, b) not in picked]
+        picked_rest = keep.tile([P, len(rest), PACK, P], F32, name="picked_rest", tag="row_sum")
+        for n, place in enumerate(rest):
+            picked[place] = picked_rest[:, n]
+        for j in range(3):
+            summed = gather_and_turn(j, [picked[j, b] for b in range(3)])
             scale_on_scalar(j, summed, early_bf[:, Q + P * j:Q + P * (j + 1), :])
-        picked = [keep.tile([P, PACK, P], F32, name=f"picked2_{b}")[:] for b in range(3)]
-        summed2 = gather_and_turn(2, picked)
+        summed3 = gather_and_turn(3, [picked[3, b] for b in range(3)])
         nc.vector.quantize_mx(out=early_codes[:].bitcast(FP8X4), scales=early_scales[:],
-                              in_=early_bf[:].rearrange("p m t -> p (m t)"))
+                              in_=early_bf[:, :Q + 2 * P, :].rearrange("p m t -> p (m t)"))
         for j in range(2):
             cols = slice(Q + P * j, Q + P * (j + 1))
             product(j, early_codes[:, cols], early_scales[:, cols])
-        store(0, 2)
-        late_bf = [keep.tile([P, P, PACK], BF16, name=f"late_bf{j}", align_bytes=64) for j in range(2)]
+        unload(0, 0)
+        weave(0, 1)
+        unload(0, 1)
+        store(0)
         late_codes = [keep.tile([P, P], U32, name=f"late_codes{j}", align_bytes=64) for j in range(2)]
         late_scales = [keep.tile([P, P], U8, name=f"late_scales{j}", align_bytes=64) for j in range(2)]
-        scale_on_scalar(2, summed2, late_bf[0][:])
-        picked = [keep.tile([P, PACK, P], F32, name=f"picked3_{b}", tag="early" if b == 2 else f"picked3_{b}",
-                            align_bytes=64)[:] for b in range(3)]
-        summed3 = gather_and_turn(3, picked)
         nc.vector.quantize_mx(out=late_codes[0][:].bitcast(FP8X4), scales=late_scales[0][:],
-                              in_=late_bf[0][:].rearrange("p m t -> p (m t)"))
+                              in_=early_bf[:, Q + 2 * P:, :].rearrange("p m t -> p (m t)"))
         product(2, late_codes[0][:], late_scales[0][:])
-        store(2, 3)
-        nc.vector.tensor_tensor(late_bf[1][:], summed3[:].rearrange("p t m -> p m t"),
+        last_bf = keep.tile([P, P, PACK], BF16, name="last_bf", tag="early", align_bytes=64)
+        nc.vector.tensor_tensor(last_bf[:], summed3[:].rearrange("p t m -> p m t"),
                                 vsc_t[:].unsqueeze(1).to_broadcast([P, P, PACK]), ALU.mult)
         nc.vector.quantize_mx(out=late_codes[1][:].bitcast(FP8X4), scales=late_scales[1][:],
-                              in_=late_bf[1][:].rearrange("p m t -> p (m t)"))
+                              in_=last_bf[:].rearrange("p m t -> p (m t)"))
         product(3, late_codes[1][:], late_scales[1][:])
-        nc.vector.tensor_copy(o_bf[:, :P, :], acc[0][:].rearrange("p t q -> p q t"))
-        nc.scalar.copy(o_bf[:, P:, :], acc[1][:].rearrange("p t q -> p q t"))
-        store(3, 4)
+        weave(0, 0)
+        weave(1, 0)
+        weave(1, 1)
+        unload(1, 1)
+        unload(1, 0)
+        store(1)
 
         o_codes = keep.tile([P, Q], U32, name="o_codes", align_bytes=64)
         o_scales = keep.tile([P, Q], U8, name="o_scales", align_bytes=64)
@@ -195,6 +210,6 @@ def tile_attend_additivekeys_pl_kernel(tc, query, ba_words, ba_scales, bb_words,
                               in_=o_bf[:].rearrange("p q t -> p (q t)"))
         nc.sync.dma_start(out_1[0].rearrange("p c t -> p (c t)").bitcast(I32), o_codes[:].bitcast(I32))
         for quad in range(4):
-            queue = nc.sync if quad % 2 == 0 else nc.scalar
+            queue = nc.sync if quad < 2 else nc.scalar
             queue.dma_start(out_2[0, 4 * quad:4 * quad + 4, :].bitcast(I32),
                             o_scales[32 * quad:32 * quad + 4, :].bitcast(I32))

@@ -39,7 +39,8 @@ def tile_attend_additivekeys_pl_kernel(tc, query, ba_words, ba_scales, bb_words,
                    keep.tile([P, WIN], I32, name="key_tab1"),
                    keep.tile([P, WIN], I32, name="key_tab2")]
         scale_tab = [keep.tile([P, WIN], U8, name=f"scale_tab{b}", tag=f"scale_tab{b}") for b in range(3)]
-        val_tab = [[keep.tile([P, U + WIN], F32, name=f"val_tab{b}_{u}") for u in range(2)] for b in range(3)]
+        val_tab = [[keep.tile([P, U + WIN], F32, name=f"val_tab{b}_{u}",
+                              tag="neg_max" if (b, u) == (0, 0) else f"val_tab{b}_{u}") for u in range(2)] for b in range(3)]
         ident = keep.tile([P, P], F32, name="ident")
 
         for b in range(3):
@@ -61,14 +62,13 @@ def tile_attend_additivekeys_pl_kernel(tc, query, ba_words, ba_scales, bb_words,
         q_raw = keep.tile([P, PACK, Q], F32, name="q_raw")
         nc.sync.dma_start(q_raw[:], query.rearrange("(p t) q -> p t q", t=PACK))
         val_rows = [table.rearrange("(p t) u -> p (t u)", t=PACK) for table in (ca, cb, cc)]
-        nc.sync.dma_start(val_tab[0][0][:, :2 * U], val_rows[0][:, :2 * U])
         for b, scales in enumerate((ba_scales, bb_scales, bc_scales)):
             for quad in range(4):
                 nc.sync.dma_start(scale_tab[b][32 * quad:32 * quad + 4, :U].bitcast(I32),
                                   scales[0, 4 * quad:4 * quad + 4, :].bitcast(I32))
         size_t = keep.tile([P, PACK], F32, name="size_t")
         vsc_t = keep.tile([P, PACK], F32, name="vsc_t")
-        for b in (1, 2):
+        for b in range(3):
             nc.sync.dma_start(val_tab[b][0][:, :2 * U], val_rows[b][:, :2 * U])
         nc.sync.dma_start(vsc_t[:], vsc.rearrange("(p t) o -> p (t o)", t=PACK))
         nc.sync.dma_start(size_t[:], size.rearrange("o (p t) -> (o p) t", t=PACK))
@@ -100,8 +100,8 @@ def tile_attend_additivekeys_pl_kernel(tc, query, ba_words, ba_scales, bb_words,
                                     rhs=key[b][:].bitcast(FP4X4 if b == 0 else FP8X4), rhs_scale=key_scale[b][:],
                                     start=(b == 0), stop=(b == 2))
 
-        neg_max = keep.tile([P, HALVES], F32, name="neg_max")
-        row_sum = keep.tile([P, HALVES], F32, name="row_sum", tag="row_sum")
+        neg_max = keep.tile([P, HALVES], F32, name="neg_max", tag="neg_max")
+        row_sum = keep.tile([P, HALVES], F32, name="row_sum")
         inv_sum = keep.tile([P, HALVES], F32, name="inv_sum")
         prob = [keep.tile([P, PACK, P], F32, name=f"prob{h}") for h in range(HALVES)]
         for h in range(HALVES):
@@ -124,8 +124,7 @@ def tile_attend_additivekeys_pl_kernel(tc, query, ba_words, ba_scales, bb_words,
         nc.scalar.copy(early_bf[:, :Q, :].rearrange("p (c i) t -> p c t i", i=4),
                        w_planes[:].rearrange("p t (c i) -> p c t i", i=4))
 
-        acc = [[psum.tile([P, 2, P], F32, name=f"acc{u}_{h}", tag=f"score{h}" if u == 0 else f"acc{h}")
-                for h in range(HALVES)] for u in range(2)]
+        acc = [psum.tile([P, PACK, P], F32, name=f"acc{h}") for h in range(HALVES)]
         o_sb = keep.tile([P, PACK, Q], F32, name="o_sb")
         o_rows = out_0.rearrange("(p t) q -> p t q", t=PACK)
         o_bf = keep.tile([P, Q, PACK], BF16, name="o_bf", align_bytes=64)
@@ -151,26 +150,26 @@ def tile_attend_additivekeys_pl_kernel(tc, query, ba_words, ba_scales, bb_words,
         def product(j, v_codes, v_scales):
             for h in range(HALVES):
                 cols = slice(P * h, P * (h + 1))
-                nc.tensor.matmul_mx(out=acc[j // 2][h][:, j % 2, :], lhsT=v_codes.bitcast(FP8X4), lhsT_scale=v_scales,
+                nc.tensor.matmul_mx(out=acc[h][:, j, :], lhsT=v_codes.bitcast(FP8X4), lhsT_scale=v_scales,
                                     rhs=early_codes[:, cols].bitcast(FP8X4), rhs_scale=early_scales[:, cols],
                                     start=True, stop=True)
 
         def unload(u, h):
-            nc.scalar.copy(o_sb[:, 2 * u:2 * u + 2, P * h:P * (h + 1)], acc[u][h][:])
+            nc.scalar.copy(o_sb[:, 2 * u:2 * u + 2, P * h:P * (h + 1)], acc[h][:, 2 * u:2 * u + 2, :])
 
-        def weave(u, h):
+        def weave(h):
             copy = nc.vector.tensor_copy if h == 0 else nc.scalar.copy
-            copy(o_bf[:, P * h:P * (h + 1), 2 * u:2 * u + 2], acc[u][h][:].rearrange("p j q -> p q j"))
+            copy(o_bf[:, P * h:P * (h + 1), :], acc[h][:].rearrange("p j q -> p q j"))
 
         def store(u):
             queue = nc.sync if u == 0 else nc.scalar
             queue.dma_start(o_rows[:, 2 * u:2 * u + 2, :], o_sb[:, 2 * u:2 * u + 2, :])
 
         picked = {(0, 0): keep.tile([P, PACK, P], F32, name="picked00")[:],
-                  (1, 0): keep.tile([P, PACK, P], F32, name="picked10", tag="scale_tab2")[:],
+                  (1, 0): keep.tile([P, PACK, P], F32, name="picked10")[:],
                   (0, 1): keep.tile([P, PACK, P], F32, name="picked01", tag="key_scale2", align_bytes=64)[:]}
         rest = [(j, b) for j in range(PACK) for b in range(3) if (j, b) not in picked]
-        picked_rest = keep.tile([P, len(rest), PACK, P], F32, name="picked_rest", tag="row_sum")
+        picked_rest = keep.tile([P, len(rest), PACK, P], F32, name="picked_rest", tag="neg_max")
         for n, place in enumerate(rest):
             picked[place] = picked_rest[:, n]
         for j in range(3):
@@ -183,7 +182,6 @@ def tile_attend_additivekeys_pl_kernel(tc, query, ba_words, ba_scales, bb_words,
             cols = slice(Q + P * j, Q + P * (j + 1))
             product(j, early_codes[:, cols], early_scales[:, cols])
         unload(0, 0)
-        weave(0, 1)
         unload(0, 1)
         store(0)
         late_codes = [keep.tile([P, P], U32, name=f"late_codes{j}", align_bytes=64) for j in range(2)]
@@ -197,9 +195,8 @@ def tile_attend_additivekeys_pl_kernel(tc, query, ba_words, ba_scales, bb_words,
         nc.vector.quantize_mx(out=late_codes[1][:].bitcast(FP8X4), scales=late_scales[1][:],
                               in_=last_bf[:].rearrange("p m t -> p (m t)"))
         product(3, late_codes[1][:], late_scales[1][:])
-        weave(0, 0)
-        weave(1, 0)
-        weave(1, 1)
+        weave(0)
+        weave(1)
         unload(1, 1)
         unload(1, 0)
         store(1)

@@ -24,7 +24,7 @@ WIN = 704
 WIN16 = 1024
 SPARE = WIN - U
 HALVES = Q // P
-START = (0, U, U, 0)
+START = (U, 0, U, 0)
 
 
 def tile_attend_additivekeys_pl_kernel(tc, query, ba_words, ba_scales, bb_words, bb_scales, bc_words, bc_scales,
@@ -62,19 +62,26 @@ def tile_attend_additivekeys_pl_kernel(tc, query, ba_words, ba_scales, bb_words,
         q_raw = keep.tile([P, PACK, Q], F32, name="q_raw")
         nc.sync.dma_start(q_raw[:], query.rearrange("(p t) q -> p t q", t=PACK))
         val_rows = [table.rearrange("(p t) u -> p (t u)", t=PACK) for table in (ca, cb, cc)]
+
+        def load_values(j, b):
+            nc.sync.dma_start(val_tab[b][j // 2][:, START[j]:START[j] + U], val_rows[b][:, U * j:U * (j + 1)])
+
+        load_values(0, 0)
         for b, scales in enumerate((ba_scales, bb_scales, bc_scales)):
             for quad in range(4):
                 nc.sync.dma_start(scale_tab[b][32 * quad:32 * quad + 4, :U].bitcast(I32),
                                   scales[0, 4 * quad:4 * quad + 4, :].bitcast(I32))
         size_t = keep.tile([P, PACK], F32, name="size_t")
         vsc_t = keep.tile([P, PACK], F32, name="vsc_t")
-        for b in range(3):
-            nc.sync.dma_start(val_tab[b][0][:, :2 * U], val_rows[b][:, :2 * U])
+        load_values(1, 0)
+        for j in range(2):
+            for b in (1, 2):
+                load_values(j, b)
         nc.sync.dma_start(vsc_t[:], vsc.rearrange("(p t) o -> p (t o)", t=PACK))
         nc.sync.dma_start(size_t[:], size.rearrange("o (p t) -> (o p) t", t=PACK))
         for j in (2, 3):
             for b in range(3):
-                nc.sync.dma_start(val_tab[b][1][:, START[j]:START[j] + U], val_rows[b][:, U * j:U * (j + 1)])
+                load_values(j, b)
 
         q_bf = keep.tile([P, Q, PACK], BF16, name="q_bf", align_bytes=64)
         nc.scalar.copy(q_bf[:].rearrange("p (c i) t -> p c t i", i=4),

@@ -53,31 +53,32 @@ def tile_attend_additivekeys_pl_kernel(tc, query, ba_words, ba_scales, bb_words,
             for b in range(3):
                 nc.gpsimd.memset(val_tab[b][u][:, 2 * U:], 0.0)
 
+        nc.sync.dma_start(key_tab[0][:, :2 * U].bitcast(I32), ba_words[0].bitcast(I32))
         nc.sync.dma_start(lists[0][:], offs)
-        nc.scalar.dma_start(key_tab[0][:, :2 * U].bitcast(I32), ba_words[0].bitcast(I32))
         nc.sync.dma_start(lists[1][:], offs2)
         nc.sync.dma_start(key_tab[1][:, :U], bb_words[0].rearrange("p n t -> p (n t)").bitcast(I32))
         nc.sync.dma_start(lists[2][:], offs3)
         nc.sync.dma_start(key_tab[2][:, :U], bc_words[0].rearrange("p n t -> p (n t)").bitcast(I32))
         q_raw = keep.tile([P, PACK, Q], F32, name="q_raw")
-        nc.sync.dma_start(q_raw[:], query.rearrange("(p t) q -> p t q", t=PACK))
         val_rows = [table.rearrange("(p t) u -> p (t u)", t=PACK) for table in (ca, cb, cc)]
 
         def load_values(j, b):
             nc.sync.dma_start(val_tab[b][j // 2][:, START[j]:START[j] + U], val_rows[b][:, U * j:U * (j + 1)])
 
         load_values(0, 0)
+        nc.sync.dma_start(q_raw[:], query.rearrange("(p t) q -> p t q", t=PACK))
+        load_values(0, 1)
+        load_values(0, 2)
+        size_t = keep.tile([P, PACK], F32, name="size_t")
+        vsc_t = keep.tile([P, PACK], F32, name="vsc_t", tag="vsc", align_bytes=64)
+        nc.sync.dma_start(vsc_t[:], vsc.rearrange("(p t) o -> p (t o)", t=PACK))
         for b, scales in enumerate((ba_scales, bb_scales, bc_scales)):
             for quad in range(4):
                 nc.sync.dma_start(scale_tab[b][32 * quad:32 * quad + 4, :U].bitcast(I32),
                                   scales[0, 4 * quad:4 * quad + 4, :].bitcast(I32))
-        size_t = keep.tile([P, PACK], F32, name="size_t")
-        vsc_t = keep.tile([P, PACK], F32, name="vsc_t")
         load_values(1, 0)
-        for j in range(2):
-            for b in (1, 2):
-                load_values(j, b)
-        nc.sync.dma_start(vsc_t[:], vsc.rearrange("(p t) o -> p (t o)", t=PACK))
+        load_values(1, 1)
+        load_values(1, 2)
         nc.sync.dma_start(size_t[:], size.rearrange("o (p t) -> (o p) t", t=PACK))
         for j in (2, 3):
             for b in range(3):
@@ -120,7 +121,7 @@ def tile_attend_additivekeys_pl_kernel(tc, query, ba_words, ba_scales, bb_words,
         early_bf = keep.tile([P, Q + 3 * P, PACK], BF16, name="early_bf", tag="early", align_bytes=64)
         early_codes = keep.tile([P, Q + 2 * P], U32, name="early_codes", align_bytes=64)
         early_scales = keep.tile([P, Q + 2 * P], U8, name="early_scales", align_bytes=64)
-        w_turned = [psum.tile([P, 2, Q], F32, name=f"w_turned{u}", tag=f"turn{u + 1}") for u in range(2)]
+        w_turned = [psum.tile([P, 2, Q], F32, name=f"w_turned{u}", tag=f"acc{u}") for u in range(2)]
         for h in range(HALVES):
             normed = keep.tile([P, PACK, P], F32, name=f"normed{h}")
             nc.scalar.activation(normed[:], prob[h][:], ACT.Copy, scale=inv_sum[:, h:h + 1])
@@ -131,10 +132,11 @@ def tile_attend_additivekeys_pl_kernel(tc, query, ba_words, ba_scales, bb_words,
         nc.scalar.copy(early_bf[:, :Q, :].rearrange("p (c i) t -> p c t i", i=4),
                        w_planes[:].rearrange("p t (c i) -> p c t i", i=4))
 
-        acc = [psum.tile([P, PACK, P], F32, name=f"acc{h}") for h in range(HALVES)]
+        acc = [[psum.tile([P, 2, P], F32, name=f"acc{u}{h}", tag=f"acc{h}" if u == 0 else f"score{h}")
+                for h in range(HALVES)] for u in range(2)]
         o_sb = keep.tile([P, PACK, Q], F32, name="o_sb")
         o_rows = out_0.rearrange("(p t) q -> p t q", t=PACK)
-        o_bf = keep.tile([P, Q, PACK], BF16, name="o_bf", align_bytes=64)
+        o_bf = keep.tile([P, Q, PACK], BF16, name="o_bf", tag="vsc", align_bytes=64)
 
         def gather_and_turn(j, picked):
             summed = psum.tile([P, PACK, P], F32, name=f"summed{j}", tag=f"turn{j % 3}")
@@ -157,24 +159,24 @@ def tile_attend_additivekeys_pl_kernel(tc, query, ba_words, ba_scales, bb_words,
         def product(j, v_codes, v_scales):
             for h in range(HALVES):
                 cols = slice(P * h, P * (h + 1))
-                nc.tensor.matmul_mx(out=acc[h][:, j, :], lhsT=v_codes.bitcast(FP8X4), lhsT_scale=v_scales,
+                nc.tensor.matmul_mx(out=acc[j // 2][h][:, j % 2, :], lhsT=v_codes.bitcast(FP8X4), lhsT_scale=v_scales,
                                     rhs=early_codes[:, cols].bitcast(FP8X4), rhs_scale=early_scales[:, cols],
                                     start=True, stop=True)
 
         def unload(u, h):
-            nc.scalar.copy(o_sb[:, 2 * u:2 * u + 2, P * h:P * (h + 1)], acc[h][:, 2 * u:2 * u + 2, :])
+            nc.scalar.copy(o_sb[:, 2 * u:2 * u + 2, P * h:P * (h + 1)], acc[u][h][:])
 
         def weave(h):
             copy = nc.vector.tensor_copy if h == 0 else nc.scalar.copy
-            copy(o_bf[:, P * h:P * (h + 1), :], acc[h][:].rearrange("p j q -> p q j"))
+            copy(o_bf[:, P * h:P * (h + 1), 2:], acc[1][h][:].rearrange("p j q -> p q j"))
 
         def store(u):
             queue = nc.sync if u == 0 else nc.scalar
             queue.dma_start(o_rows[:, 2 * u:2 * u + 2, :], o_sb[:, 2 * u:2 * u + 2, :])
 
-        picked = {(0, 0): keep.tile([P, PACK, P], F32, name="picked00")[:],
-                  (1, 0): keep.tile([P, PACK, P], F32, name="picked10")[:],
-                  (0, 1): keep.tile([P, PACK, P], F32, name="picked01", tag="key_scale2", align_bytes=64)[:]}
+        picked = {place: keep.tile([P, PACK, P], F32, name=f"picked{place[0]}{place[1]}")[:]
+                  for place in ((0, 0), (0, 1), (0, 2), (1, 0))}
+        picked[1, 1] = keep.tile([P, PACK, P], F32, name="picked11", tag="key_scale2", align_bytes=64)[:]
         rest = [(j, b) for j in range(PACK) for b in range(3) if (j, b) not in picked]
         picked_rest = keep.tile([P, len(rest), PACK, P], F32, name="picked_rest", tag="neg_max")
         for n, place in enumerate(rest):
@@ -202,6 +204,7 @@ def tile_attend_additivekeys_pl_kernel(tc, query, ba_words, ba_scales, bb_words,
         nc.vector.quantize_mx(out=late_codes[1][:].bitcast(FP8X4), scales=late_scales[1][:],
                               in_=last_bf[:].rearrange("p m t -> p (m t)"))
         product(3, late_codes[1][:], late_scales[1][:])
+        nc.vector.tensor_copy(o_bf[:, :, :2], o_sb[:, :2, :].rearrange("p j q -> p q j"))
         weave(0)
         weave(1)
         unload(1, 1)

@@ -39,8 +39,7 @@ def tile_attend_additivekeys_pl_kernel(tc, query, ba_words, ba_scales, bb_words,
                    keep.tile([P, WIN], I32, name="key_tab1"),
                    keep.tile([P, WIN], I32, name="key_tab2")]
         scale_tab = [keep.tile([P, WIN], U8, name=f"scale_tab{b}", tag=f"scale_tab{b}") for b in range(3)]
-        val_tab = [[keep.tile([P, U + WIN], F32, name=f"val_tab{b}_{u}",
-                              tag="neg_max" if (b, u) == (0, 0) else f"val_tab{b}_{u}") for u in range(2)] for b in range(3)]
+        val_tab = [[keep.tile([P, U + WIN], F32, name=f"val_tab{b}_{u}") for u in range(2)] for b in range(3)]
         ident = keep.tile([P, P], F32, name="ident")
 
         for b in range(3):
@@ -54,11 +53,10 @@ def tile_attend_additivekeys_pl_kernel(tc, query, ba_words, ba_scales, bb_words,
                 nc.gpsimd.memset(val_tab[b][u][:, 2 * U:], 0.0)
 
         nc.sync.dma_start(key_tab[0][:, :2 * U].bitcast(I32), ba_words[0].bitcast(I32))
-        nc.sync.dma_start(lists[0][:], offs)
-        nc.sync.dma_start(lists[1][:], offs2)
-        nc.sync.dma_start(key_tab[1][:, :U], bb_words[0].rearrange("p n t -> p (n t)").bitcast(I32))
-        nc.sync.dma_start(lists[2][:], offs3)
-        nc.sync.dma_start(key_tab[2][:, :U], bc_words[0].rearrange("p n t -> p (n t)").bitcast(I32))
+        for b, offsets in enumerate((offs, offs2, offs3)):
+            nc.sync.dma_start(lists[b][:], offsets)
+        for b, words in ((1, bb_words), (2, bc_words)):
+            nc.sync.dma_start(key_tab[b][:, :U], words[0].rearrange("p n t -> p (n t)").bitcast(I32))
         q_raw = keep.tile([P, PACK, Q], F32, name="q_raw")
         val_rows = [table.rearrange("(p t) u -> p (t u)", t=PACK) for table in (ca, cb, cc)]
 
@@ -67,20 +65,17 @@ def tile_attend_additivekeys_pl_kernel(tc, query, ba_words, ba_scales, bb_words,
 
         load_values(0, 0)
         nc.sync.dma_start(q_raw[:], query.rearrange("(p t) q -> p t q", t=PACK))
-        load_values(0, 1)
-        load_values(0, 2)
-        size_t = keep.tile([P, PACK], F32, name="size_t")
-        vsc_t = keep.tile([P, PACK], F32, name="vsc_t", tag="vsc", align_bytes=64)
-        nc.sync.dma_start(vsc_t[:], vsc.rearrange("(p t) o -> p (t o)", t=PACK))
         for b, scales in enumerate((ba_scales, bb_scales, bc_scales)):
             for quad in range(4):
                 nc.sync.dma_start(scale_tab[b][32 * quad:32 * quad + 4, :U].bitcast(I32),
                                   scales[0, 4 * quad:4 * quad + 4, :].bitcast(I32))
-        load_values(1, 0)
-        load_values(1, 1)
-        load_values(1, 2)
+        size_t = keep.tile([P, PACK], F32, name="size_t")
+        vsc_t = keep.tile([P, PACK], F32, name="vsc_t", tag="vsc", align_bytes=64)
+        load_values(0, 1)
+        load_values(0, 2)
+        nc.sync.dma_start(vsc_t[:], vsc.rearrange("(p t) o -> p (t o)", t=PACK))
         nc.sync.dma_start(size_t[:], size.rearrange("o (p t) -> (o p) t", t=PACK))
-        for j in (2, 3):
+        for j in (1, 2, 3):
             for b in range(3):
                 load_values(j, b)
 
@@ -132,8 +127,8 @@ def tile_attend_additivekeys_pl_kernel(tc, query, ba_words, ba_scales, bb_words,
         nc.scalar.copy(early_bf[:, :Q, :].rearrange("p (c i) t -> p c t i", i=4),
                        w_planes[:].rearrange("p t (c i) -> p c t i", i=4))
 
-        acc = [[psum.tile([P, 2, P], F32, name=f"acc{u}{h}", tag=f"acc{h}" if u == 0 else f"score{h}")
-                for h in range(HALVES)] for u in range(2)]
+        acc_early = [psum.tile([P, Q], F32, name=f"acc_early{j}", tag=f"acc{j}") for j in range(2)]
+        acc = [psum.tile([P, 2, P], F32, name=f"acc_late{h}", tag=f"score{h}") for h in range(HALVES)]
         o_sb = keep.tile([P, PACK, Q], F32, name="o_sb")
         o_rows = out_0.rearrange("(p t) q -> p t q", t=PACK)
         o_bf = keep.tile([P, Q, PACK], BF16, name="o_bf", tag="vsc", align_bytes=64)
@@ -159,24 +154,24 @@ def tile_attend_additivekeys_pl_kernel(tc, query, ba_words, ba_scales, bb_words,
         def product(j, v_codes, v_scales):
             for h in range(HALVES):
                 cols = slice(P * h, P * (h + 1))
-                nc.tensor.matmul_mx(out=acc[j // 2][h][:, j % 2, :], lhsT=v_codes.bitcast(FP8X4), lhsT_scale=v_scales,
+                nc.tensor.matmul_mx(out=acc[h][:, j % 2, :], lhsT=v_codes.bitcast(FP8X4), lhsT_scale=v_scales,
                                     rhs=early_codes[:, cols].bitcast(FP8X4), rhs_scale=early_scales[:, cols],
                                     start=True, stop=True)
 
-        def unload(u, h):
-            nc.scalar.copy(o_sb[:, 2 * u:2 * u + 2, P * h:P * (h + 1)], acc[u][h][:])
+        def unload(h):
+            nc.scalar.copy(o_sb[:, 2:, P * h:P * (h + 1)], acc[h][:])
 
         def weave(h):
             copy = nc.vector.tensor_copy if h == 0 else nc.scalar.copy
-            copy(o_bf[:, P * h:P * (h + 1), 2:], acc[1][h][:].rearrange("p j q -> p q j"))
+            copy(o_bf[:, P * h:P * (h + 1), 2:], acc[h][:].rearrange("p j q -> p q j"))
 
         def store(u):
             queue = nc.sync if u == 0 else nc.scalar
             queue.dma_start(o_rows[:, 2 * u:2 * u + 2, :], o_sb[:, 2 * u:2 * u + 2, :])
 
         picked = {place: keep.tile([P, PACK, P], F32, name=f"picked{place[0]}{place[1]}")[:]
-                  for place in ((0, 0), (0, 1), (0, 2), (1, 0))}
-        picked[1, 1] = keep.tile([P, PACK, P], F32, name="picked11", tag="key_scale2", align_bytes=64)[:]
+                  for place in ((0, 0), (0, 1))}
+        picked[0, 2] = keep.tile([P, PACK, P], F32, name="picked02", tag="key_scale2", align_bytes=64)[:]
         rest = [(j, b) for j in range(PACK) for b in range(3) if (j, b) not in picked]
         picked_rest = keep.tile([P, len(rest), PACK, P], F32, name="picked_rest", tag="neg_max")
         for n, place in enumerate(rest):
@@ -189,9 +184,10 @@ def tile_attend_additivekeys_pl_kernel(tc, query, ba_words, ba_scales, bb_words,
                               in_=early_bf[:, :Q + 2 * P, :].rearrange("p m t -> p (m t)"))
         for j in range(2):
             cols = slice(Q + P * j, Q + P * (j + 1))
-            product(j, early_codes[:, cols], early_scales[:, cols])
-        unload(0, 0)
-        unload(0, 1)
+            nc.tensor.matmul_mx(out=acc_early[j][:], lhsT=early_codes[:, cols].bitcast(FP8X4),
+                                lhsT_scale=early_scales[:, cols], rhs=early_codes[:, :Q].bitcast(FP8X4),
+                                rhs_scale=early_scales[:, :Q], start=True, stop=True)
+            nc.scalar.copy(o_sb[:, j, :], acc_early[j][:])
         store(0)
         late_codes = [keep.tile([P, P], U32, name=f"late_codes{j}", align_bytes=64) for j in range(2)]
         late_scales = [keep.tile([P, P], U8, name=f"late_scales{j}", align_bytes=64) for j in range(2)]
@@ -207,14 +203,16 @@ def tile_attend_additivekeys_pl_kernel(tc, query, ba_words, ba_scales, bb_words,
         nc.vector.tensor_copy(o_bf[:, :, :2], o_sb[:, :2, :].rearrange("p j q -> p q j"))
         weave(0)
         weave(1)
-        unload(1, 1)
-        unload(1, 0)
+        unload(1)
+        unload(0)
         store(1)
 
         o_codes = keep.tile([P, Q], U32, name="o_codes", align_bytes=64)
         o_scales = keep.tile([P, Q], U8, name="o_scales", align_bytes=64)
-        nc.vector.quantize_mx(out=o_codes[:].bitcast(FP8X4), scales=o_scales[:],
-                              in_=o_bf[:].rearrange("p q t -> p (q t)"))
+        for h in (1, 0):
+            cols = slice(P * h, P * (h + 1))
+            nc.vector.quantize_mx(out=o_codes[:, cols].bitcast(FP8X4), scales=o_scales[:, cols],
+                                  in_=o_bf[:, cols, :].rearrange("p q t -> p (q t)"))
         nc.sync.dma_start(out_1[0].rearrange("p c t -> p (c t)").bitcast(I32), o_codes[:].bitcast(I32))
         for quad in range(4):
             queue = nc.sync if quad < 2 else nc.scalar

@@ -20,11 +20,11 @@ AXIS = mybir.AxisListType
 
 P = 128
 PACK = 4
-WIN = 704
+WIN = 688
 WIN16 = 1024
 SPARE = WIN - U
 HALVES = Q // P
-START = (U, 0, U, 0)
+START = tuple(U * (PACK - 1 - j) for j in range(PACK))
 
 
 def tile_attend_additivekeys_pl_kernel(tc, query, ba_words, ba_scales, bb_words, bb_scales, bc_words, bc_scales,
@@ -39,18 +39,17 @@ def tile_attend_additivekeys_pl_kernel(tc, query, ba_words, ba_scales, bb_words,
                    keep.tile([P, WIN], I32, name="key_tab1"),
                    keep.tile([P, WIN], I32, name="key_tab2")]
         scale_tab = [keep.tile([P, WIN], U8, name=f"scale_tab{b}", tag=f"scale_tab{b}") for b in range(3)]
-        val_tab = [[keep.tile([P, U + WIN], F32, name=f"val_tab{b}_{u}") for u in range(2)] for b in range(3)]
+        val_tab = [keep.tile([P, PACK * U + SPARE], F32, name=f"val_tab{b}") for b in range(3)]
         ident = keep.tile([P, P], F32, name="ident")
 
+        nc.vector.memset(key_tab[0][:, 2 * U:].bitcast(I32), 0)
         for b in range(3):
             nc.vector.memset(scale_tab[b][:].bitcast(I32), 0)
-        nc.vector.memset(key_tab[0][:, 2 * U:].bitcast(I32), 0)
         for b in (1, 2):
             nc.vector.memset(key_tab[b][:, U:], 0)
+        for b in range(3):
+            nc.vector.memset(val_tab[b][:, PACK * U:], 0.0)
         make_identity(nc, ident[:])
-        for u in range(2):
-            for b in range(3):
-                nc.gpsimd.memset(val_tab[b][u][:, 2 * U:], 0.0)
 
         nc.sync.dma_start(key_tab[0][:, :2 * U].bitcast(I32), ba_words[0].bitcast(I32))
         for b, offsets in enumerate((offs, offs2, offs3)):
@@ -61,7 +60,7 @@ def tile_attend_additivekeys_pl_kernel(tc, query, ba_words, ba_scales, bb_words,
         val_rows = [table.rearrange("(p t) u -> p (t u)", t=PACK) for table in (ca, cb, cc)]
 
         def load_values(j, b):
-            nc.sync.dma_start(val_tab[b][j // 2][:, START[j]:START[j] + U], val_rows[b][:, U * j:U * (j + 1)])
+            nc.sync.dma_start(val_tab[b][:, START[j]:START[j] + U], val_rows[b][:, U * j:U * (j + 1)])
 
         load_values(0, 0)
         nc.sync.dma_start(q_raw[:], query.rearrange("(p t) q -> p t q", t=PACK))
@@ -136,7 +135,7 @@ def tile_attend_additivekeys_pl_kernel(tc, query, ba_words, ba_scales, bb_words,
         def gather_and_turn(j, picked):
             summed = psum.tile([P, PACK, P], F32, name=f"summed{j}", tag=f"turn{j % 3}")
             for b in range(3):
-                window = val_tab[b][j // 2][:, START[j]:START[j] + WIN]
+                window = val_tab[b][:, START[j]:START[j] + WIN]
                 nc.vector.tensor_copy(picked[b].bitcast(U32).rearrange("p t s -> p s t"),
                                       window.bitcast(U32).indirect(lists[b][:]))
                 for t in range(PACK):

@@ -20,11 +20,11 @@ AXIS = mybir.AxisListType
 
 P = 128
 PACK = 4
-WIN = 688
+WIN = 704
 WIN16 = 1024
 SPARE = WIN - U
 HALVES = Q // P
-START = tuple(U * (PACK - 1 - j) for j in range(PACK))
+START = (U, 0, U, 0)
 
 
 def tile_attend_additivekeys_pl_kernel(tc, query, ba_words, ba_scales, bb_words, bb_scales, bc_words, bc_scales,
@@ -39,17 +39,18 @@ def tile_attend_additivekeys_pl_kernel(tc, query, ba_words, ba_scales, bb_words,
                    keep.tile([P, WIN], I32, name="key_tab1"),
                    keep.tile([P, WIN], I32, name="key_tab2")]
         scale_tab = [keep.tile([P, WIN], U8, name=f"scale_tab{b}", tag=f"scale_tab{b}") for b in range(3)]
-        val_tab = [keep.tile([P, PACK * U + SPARE], F32, name=f"val_tab{b}") for b in range(3)]
+        val_tab = [[keep.tile([P, U + WIN], F32, name=f"val_tab{b}_{u}") for u in range(2)] for b in range(3)]
         ident = keep.tile([P, P], F32, name="ident")
 
-        nc.vector.memset(key_tab[0][:, 2 * U:].bitcast(I32), 0)
         for b in range(3):
             nc.vector.memset(scale_tab[b][:].bitcast(I32), 0)
+        nc.vector.memset(key_tab[0][:, 2 * U:].bitcast(I32), 0)
         for b in (1, 2):
             nc.vector.memset(key_tab[b][:, U:], 0)
-        for b in range(3):
-            nc.vector.memset(val_tab[b][:, PACK * U:], 0.0)
         make_identity(nc, ident[:])
+        for u in range(2):
+            for b in range(3):
+                nc.gpsimd.memset(val_tab[b][u][:, 2 * U:], 0.0)
 
         nc.sync.dma_start(key_tab[0][:, :2 * U].bitcast(I32), ba_words[0].bitcast(I32))
         for b, offsets in enumerate((offs, offs2, offs3)):
@@ -60,7 +61,7 @@ def tile_attend_additivekeys_pl_kernel(tc, query, ba_words, ba_scales, bb_words,
         val_rows = [table.rearrange("(p t) u -> p (t u)", t=PACK) for table in (ca, cb, cc)]
 
         def load_values(j, b):
-            nc.sync.dma_start(val_tab[b][:, START[j]:START[j] + U], val_rows[b][:, U * j:U * (j + 1)])
+            nc.sync.dma_start(val_tab[b][j // 2][:, START[j]:START[j] + U], val_rows[b][:, U * j:U * (j + 1)])
 
         load_values(0, 0)
         nc.sync.dma_start(q_raw[:], query.rearrange("(p t) q -> p t q", t=PACK))
@@ -126,7 +127,7 @@ def tile_attend_additivekeys_pl_kernel(tc, query, ba_words, ba_scales, bb_words,
         nc.scalar.copy(early_bf[:, :Q, :].rearrange("p (c i) t -> p c t i", i=4),
                        w_planes[:].rearrange("p t (c i) -> p c t i", i=4))
 
-        acc_early = [psum.tile([P, Q], F32, name=f"acc_early{j}", tag=f"acc{j}") for j in range(2)]
+        acc_early = [psum.tile([P, 2, P], F32, name=f"acc_early{h}", tag=f"acc{h}") for h in range(HALVES)]
         acc = [psum.tile([P, 2, P], F32, name=f"acc_late{h}", tag=f"score{h}") for h in range(HALVES)]
         o_sb = keep.tile([P, PACK, Q], F32, name="o_sb")
         o_rows = out_0.rearrange("(p t) q -> p t q", t=PACK)
@@ -135,7 +136,7 @@ def tile_attend_additivekeys_pl_kernel(tc, query, ba_words, ba_scales, bb_words,
         def gather_and_turn(j, picked):
             summed = psum.tile([P, PACK, P], F32, name=f"summed{j}", tag=f"turn{j % 3}")
             for b in range(3):
-                window = val_tab[b][:, START[j]:START[j] + WIN]
+                window = val_tab[b][j // 2][:, START[j]:START[j] + WIN]
                 nc.vector.tensor_copy(picked[b].bitcast(U32).rearrange("p t s -> p s t"),
                                       window.bitcast(U32).indirect(lists[b][:]))
                 for t in range(PACK):
@@ -158,7 +159,8 @@ def tile_attend_additivekeys_pl_kernel(tc, query, ba_words, ba_scales, bb_words,
                                     start=True, stop=True)
 
         def unload(h):
-            nc.scalar.copy(o_sb[:, 2:, P * h:P * (h + 1)], acc[h][:])
+            copy = nc.vector.tensor_copy if h == 0 else nc.scalar.copy
+            copy(o_sb[:, 2:, P * h:P * (h + 1)], acc[h][:])
 
         def weave(h):
             copy = nc.vector.tensor_copy if h == 0 else nc.scalar.copy
@@ -181,12 +183,14 @@ def tile_attend_additivekeys_pl_kernel(tc, query, ba_words, ba_scales, bb_words,
         summed3 = gather_and_turn(3, [picked[3, b] for b in range(3)])
         nc.vector.quantize_mx(out=early_codes[:].bitcast(FP8X4), scales=early_scales[:],
                               in_=early_bf[:, :Q + 2 * P, :].rearrange("p m t -> p (m t)"))
-        for j in range(2):
-            cols = slice(Q + P * j, Q + P * (j + 1))
-            nc.tensor.matmul_mx(out=acc_early[j][:], lhsT=early_codes[:, cols].bitcast(FP8X4),
-                                lhsT_scale=early_scales[:, cols], rhs=early_codes[:, :Q].bitcast(FP8X4),
-                                rhs_scale=early_scales[:, :Q], start=True, stop=True)
-            nc.scalar.copy(o_sb[:, j, :], acc_early[j][:])
+        for h in range(HALVES):
+            rows = slice(P * h, P * (h + 1))
+            for j in range(2):
+                cols = slice(Q + P * j, Q + P * (j + 1))
+                nc.tensor.matmul_mx(out=acc_early[h][:, j, :], lhsT=early_codes[:, cols].bitcast(FP8X4),
+                                    lhsT_scale=early_scales[:, cols], rhs=early_codes[:, rows].bitcast(FP8X4),
+                                    rhs_scale=early_scales[:, rows], start=True, stop=True)
+            nc.scalar.copy(o_sb[:, :2, rows], acc_early[h][:])
         store(0)
         late_codes = [keep.tile([P, P], U32, name=f"late_codes{j}", align_bytes=64) for j in range(2)]
         late_scales = [keep.tile([P, P], U8, name=f"late_scales{j}", align_bytes=64) for j in range(2)]
@@ -199,16 +203,17 @@ def tile_attend_additivekeys_pl_kernel(tc, query, ba_words, ba_scales, bb_words,
         nc.vector.quantize_mx(out=late_codes[1][:].bitcast(FP8X4), scales=late_scales[1][:],
                               in_=last_bf[:].rearrange("p m t -> p (m t)"))
         product(3, late_codes[1][:], late_scales[1][:])
-        nc.vector.tensor_copy(o_bf[:, :, :2], o_sb[:, :2, :].rearrange("p j q -> p q j"))
-        weave(0)
-        weave(1)
-        unload(1)
-        unload(0)
+        for h in range(HALVES):
+            rows = slice(P * h, P * (h + 1))
+            nc.vector.tensor_copy(o_bf[:, rows, :2], o_sb[:, :2, rows].rearrange("p j q -> p q j"))
+        for h in range(HALVES):
+            weave(h)
+            unload(h)
         store(1)
 
         o_codes = keep.tile([P, Q], U32, name="o_codes", align_bytes=64)
         o_scales = keep.tile([P, Q], U8, name="o_scales", align_bytes=64)
-        for h in (1, 0):
+        for h in range(HALVES):
             cols = slice(P * h, P * (h + 1))
             nc.vector.quantize_mx(out=o_codes[:, cols].bitcast(FP8X4), scales=o_scales[:, cols],
                                   in_=o_bf[:, cols, :].rearrange("p q t -> p (q t)"))

@@ -45,9 +45,9 @@ def tile_attend_additivekeys_pl_kernel(tc, query, ba_words, ba_scales, bb_words,
         for b in range(3):
             nc.vector.memset(scale_tab[b][:].bitcast(I32), 0)
         nc.vector.memset(key_tab[0][:, 2 * U:].bitcast(I32), 0)
-        for b in (1, 2):
-            nc.vector.memset(key_tab[b][:, U:], 0)
         make_identity(nc, ident[:])
+        for b in (1, 2):
+            nc.gpsimd.memset(key_tab[b][:, U:], 0)
         for u in range(2):
             for b in range(3):
                 nc.gpsimd.memset(val_tab[b][u][:, 2 * U:], 0.0)

@@ -134,20 +134,25 @@ def tile_attend_additivekeys_pl_kernel(tc, query, ba_words, ba_scales, bb_words,
         o_bf = keep.tile([P, Q, PACK], BF16, name="o_bf", tag="vsc", align_bytes=64)
 
         def gather_and_turn(j, picked):
-            summed = psum.tile([P, PACK, P], F32, name=f"summed{j}", tag=f"turn{j % 3}")
+            if j == 2:
+                pairs = [psum.tile([P, 2, P], F32, name=f"summed{j}_{u}", tag=f"turn{2 * u}") for u in range(2)]
+                summed, group = [pairs[t // 2][:, t % 2, :] for t in range(PACK)], 2
+            else:
+                whole = psum.tile([P, PACK, P], F32, name=f"summed{j}", tag=f"turn{min(j, 2)}")
+                summed, group = [whole[:, t, :] for t in range(PACK)], PACK
             for b in range(3):
                 window = val_tab[b][j // 2][:, START[j]:START[j] + WIN]
                 nc.vector.tensor_copy(picked[b].bitcast(U32).rearrange("p t s -> p s t"),
                                       window.bitcast(U32).indirect(lists[b][:]))
                 for t in range(PACK):
-                    nc.tensor.matmul(summed[:, t, :], lhsT=picked[b][:, t, :], rhs=ident[:], is_transpose=True,
-                                     start=(b == 0 and t == 0), stop=(b == 2 and t == PACK - 1))
-            return summed
+                    nc.tensor.matmul(summed[t], lhsT=picked[b][:, t, :], rhs=ident[:], is_transpose=True,
+                                     start=(b == 0 and t % group == 0), stop=(b == 2 and t % group == group - 1))
+            return whole if j == PACK - 1 else summed
 
         def scale_on_scalar(j, summed, v_bf):
             v_planes = keep.tile([P, PACK, P], BF16, name=f"v_planes{j}")
             for t in range(PACK):
-                nc.scalar.activation(v_planes[:, t, :], summed[:, t, :], ACT.Copy, scale=vsc_t[:, t:t + 1])
+                nc.scalar.activation(v_planes[:, t, :], summed[t], ACT.Copy, scale=vsc_t[:, t:t + 1])
             nc.scalar.copy(v_bf.rearrange("p (c i) t -> p c t i", i=4),
                            v_planes[:].rearrange("p t (c i) -> p c t i", i=4))
 
@@ -180,6 +185,10 @@ def tile_attend_additivekeys_pl_kernel(tc, query, ba_words, ba_scales, bb_words,
         for j in range(3):
             summed = gather_and_turn(j, [picked[j, b] for b in range(3)])
             scale_on_scalar(j, summed, early_bf[:, Q + P * j:Q + P * (j + 1), :])
+        warm = psum.tile([P, I], F32, name="warm", tag="turn0")
+        for n in range(2):
+            nc.tensor.matmul_mx(out=warm[:], lhsT=q_codes[:, :P].bitcast(FP8X4), lhsT_scale=q_scales[:, :P],
+                                rhs=key[1][:].bitcast(FP8X4), rhs_scale=key_scale[1][:], start=(n == 0), stop=(n == 1))
         summed3 = gather_and_turn(3, [picked[3, b] for b in range(3)])
         nc.vector.quantize_mx(out=early_codes[:].bitcast(FP8X4), scales=early_scales[:],
                               in_=early_bf[:, :Q + 2 * P, :].rearrange("p m t -> p (m t)"))

@@ -135,18 +135,19 @@ def tile_attend_additivekeys_pl_kernel(tc, query, ba_words, ba_scales, bb_words,
 
         def gather_and_turn(j, picked):
             if j == 2:
-                pairs = [psum.tile([P, 2, P], F32, name=f"summed{j}_{u}", tag=f"turn{2 * u}") for u in range(2)]
-                summed, group = [pairs[t // 2][:, t % 2, :] for t in range(PACK)], 2
+                first = psum.tile([P, P], F32, name="summed2_first", tag="turn0")
+                others = psum.tile([P, PACK - 1, P], F32, name="summed2_others", tag="turn2")
+                summed, opens, closes = [first[:]] + [others[:, t, :] for t in range(PACK - 1)], (0, 1), (0, PACK - 1)
             else:
                 whole = psum.tile([P, PACK, P], F32, name=f"summed{j}", tag=f"turn{min(j, 2)}")
-                summed, group = [whole[:, t, :] for t in range(PACK)], PACK
+                summed, opens, closes = [whole[:, t, :] for t in range(PACK)], (0,), (PACK - 1,)
             for b in range(3):
                 window = val_tab[b][j // 2][:, START[j]:START[j] + WIN]
                 nc.vector.tensor_copy(picked[b].bitcast(U32).rearrange("p t s -> p s t"),
                                       window.bitcast(U32).indirect(lists[b][:]))
                 for t in range(PACK):
                     nc.tensor.matmul(summed[t], lhsT=picked[b][:, t, :], rhs=ident[:], is_transpose=True,
-                                     start=(b == 0 and t % group == 0), stop=(b == 2 and t % group == group - 1))
+                                     start=(b == 0 and t in opens), stop=(b == 2 and t in closes))
             return whole if j == PACK - 1 else summed
 
         def scale_on_scalar(j, summed, v_bf):

@@ -177,8 +177,8 @@ def tile_attend_additivekeys_pl_kernel(tc, query, ba_words, ba_scales, bb_words,
             queue.dma_start(o_rows[:, 2 * u:2 * u + 2, :], o_sb[:, 2 * u:2 * u + 2, :])
 
         picked = {place: keep.tile([P, PACK, P], F32, name=f"picked{place[0]}{place[1]}")[:]
-                  for place in ((0, 0), (0, 1))}
-        picked[0, 2] = keep.tile([P, PACK, P], F32, name="picked02", tag="key_scale2", align_bytes=64)[:]
+                  for place in ((0, 0), (0, 1), (0, 2))}
+        picked[1, 0] = keep.tile([P, PACK, P], F32, name="picked10", tag="key_scale2", align_bytes=64)[:]
         rest = [(j, b) for j in range(PACK) for b in range(3) if (j, b) not in picked]
         picked_rest = keep.tile([P, len(rest), PACK, P], F32, name="picked_rest", tag="neg_max")
         for n, place in enumerate(rest):

@@ -20,11 +20,13 @@ AXIS = mybir.AxisListType
 
 P = 128
 PACK = 4
+BOOKS = 3
 WIN = 704
 WIN16 = 1024
-SPARE = WIN - U
+WIN_SCALAR = U + 8
 HALVES = Q // P
-START = (U, 0, U, 0)
+ON_VECTOR = ((2, 2), (3, 2))
+FOLLOWS = {(3, 1): "val_tab12", (3, 2): "prob1"}
 
 
 def tile_attend_additivekeys_pl_kernel(tc, query, ba_words, ba_scales, bb_words, bb_scales, bc_words, bc_scales,
@@ -34,128 +36,159 @@ def tile_attend_additivekeys_pl_kernel(tc, query, ba_words, ba_scales, bb_words,
         keep = ctx.enter_context(tc.tile_pool(name="keep", bufs=1))
         psum = ctx.enter_context(tc.psum_pool(name="psum", bufs=1))
 
-        lists = [keep.tile([P, I // 16], U16, name=f"list{b}") for b in range(3)]
+        places = [(j, b) for j in range(PACK) for b in range(BOOKS)]
+        lists = [keep.tile([P, I // 16], U16, name=f"list{b}") for b in range(BOOKS)]
         key_tab = [keep.tile([P, 2 * WIN16], U8, name="key_tab0"),
                    keep.tile([P, WIN], I32, name="key_tab1"),
                    keep.tile([P, WIN], I32, name="key_tab2")]
-        scale_tab = [keep.tile([P, WIN], U8, name=f"scale_tab{b}", tag=f"scale_tab{b}") for b in range(3)]
-        val_tab = [[keep.tile([P, U + WIN], F32, name=f"val_tab{b}_{u}") for u in range(2)] for b in range(3)]
+        scale_tab = [keep.tile([P, WIN], U8, name=f"scale_tab{b}", tag=f"scale_tab{b}", align_bytes=64) for b in range(BOOKS)]
+        val_tab = {(j, b): keep.tile([P, WIN if (j, b) in ON_VECTOR else WIN_SCALAR], F32, name=f"val_tab{j}{b}",
+                                     tag=f"val_tab{j}{b}")
+                   for j, b in places}
         ident = keep.tile([P, P], F32, name="ident")
 
-        for b in range(3):
+        warm = keep.tile([P, 2], F32, name="warm")
+        nc.gpsimd.memset(warm[:, :1], 0.0)
+        nc.scalar.activation(warm[:, 1:], warm[:, :1], ACT.Exp)
+        for b in range(BOOKS):
             nc.vector.memset(scale_tab[b][:].bitcast(I32), 0)
         nc.vector.memset(key_tab[0][:, 2 * U:].bitcast(I32), 0)
-        make_identity(nc, ident[:])
         for b in (1, 2):
-            nc.gpsimd.memset(key_tab[b][:, U:], 0)
-        for u in range(2):
-            for b in range(3):
-                nc.gpsimd.memset(val_tab[b][u][:, 2 * U:], 0.0)
+            nc.vector.memset(key_tab[b][:, U:], 0)
+        nc.gpsimd.memset(val_tab[places[0]][:, U:], 0.0)
+        make_identity(nc, ident[:])
+        for place in places[1:]:
+            nc.gpsimd.memset(val_tab[place][:, U:], 0.0)
 
-        nc.sync.dma_start(key_tab[0][:, :2 * U].bitcast(I32), ba_words[0].bitcast(I32))
-        for b, offsets in enumerate((offs, offs2, offs3)):
-            nc.sync.dma_start(lists[b][:], offsets)
-        for b, words in ((1, bb_words), (2, bc_words)):
-            nc.sync.dma_start(key_tab[b][:, :U], words[0].rearrange("p n t -> p (n t)").bitcast(I32))
         q_raw = keep.tile([P, PACK, Q], F32, name="q_raw")
+        size_t = keep.tile([P, PACK], F32, name="size_t")
+        vsc_t = keep.tile([P, PACK], F32, name="vsc_t", tag="vsc", align_bytes=64)
         val_rows = [table.rearrange("(p t) u -> p (t u)", t=PACK) for table in (ca, cb, cc)]
 
         def load_values(j, b):
-            nc.sync.dma_start(val_tab[b][j // 2][:, START[j]:START[j] + U], val_rows[b][:, U * j:U * (j + 1)])
+            nc.sync.dma_start(val_tab[j, b][:, :U], val_rows[b][:, U * j:U * (j + 1)])
 
-        load_values(0, 0)
-        nc.sync.dma_start(q_raw[:], query.rearrange("(p t) q -> p t q", t=PACK))
-        for b, scales in enumerate((ba_scales, bb_scales, bc_scales)):
+        def load_keys(b, words):
+            nc.sync.dma_start(key_tab[b][:, :U], words[0].rearrange("p n t -> p (n t)").bitcast(I32))
+
+        def load_scales(b, scales):
             for quad in range(4):
                 nc.sync.dma_start(scale_tab[b][32 * quad:32 * quad + 4, :U].bitcast(I32),
                                   scales[0, 4 * quad:4 * quad + 4, :].bitcast(I32))
-        size_t = keep.tile([P, PACK], F32, name="size_t")
-        vsc_t = keep.tile([P, PACK], F32, name="vsc_t", tag="vsc", align_bytes=64)
+
+        nc.sync.dma_start(key_tab[0][:, :2 * U].bitcast(I32), ba_words[0].bitcast(I32))
+        nc.sync.dma_start(lists[0][:], offs)
+        load_values(0, 0)
+        nc.sync.dma_start(lists[1][:], offs2)
+        load_keys(1, bb_words)
         load_values(0, 1)
+        load_keys(2, bc_words)
+        nc.sync.dma_start(lists[2][:], offs3)
+        load_scales(0, ba_scales)
         load_values(0, 2)
+        nc.sync.dma_start(q_raw[:], query.rearrange("(p t) q -> p t q", t=PACK))
+        load_values(1, 0)
+        load_scales(1, bb_scales)
+        load_values(1, 1)
         nc.sync.dma_start(vsc_t[:], vsc.rearrange("(p t) o -> p (t o)", t=PACK))
         nc.sync.dma_start(size_t[:], size.rearrange("o (p t) -> (o p) t", t=PACK))
-        for j in (1, 2, 3):
-            for b in range(3):
-                load_values(j, b)
-
-        q_bf = keep.tile([P, Q, PACK], BF16, name="q_bf", align_bytes=64)
-        nc.scalar.copy(q_bf[:].rearrange("p (c i) t -> p c t i", i=4),
-                       q_raw[:].rearrange("p t (c i) -> p c t i", i=4))
-        q_codes = keep.tile([P, Q], U32, name="q_codes", align_bytes=64)
-        q_scales = keep.tile([P, Q], U8, name="q_scales", align_bytes=64)
-        nc.vector.quantize_mx(out=q_codes[:].bitcast(FP8X4), scales=q_scales[:],
-                              in_=q_bf[:].rearrange("p q t -> p (q t)"))
+        load_values(2, 0)
+        load_scales(2, bc_scales)
+        load_values(2, 2)
+        load_values(1, 2)
+        load_values(2, 1)
+        for place in places[9:]:
+            load_values(*place)
 
         key = [keep.tile([P, 2 * I], U8, name="key0", align_bytes=64),
                keep.tile([P, I], U32, name="key1", align_bytes=64),
                keep.tile([P, I], U32, name="key2", align_bytes=64)]
-        key_scale = [keep.tile([P, I], U8, name=f"key_scale{b}", tag=f"key_scale{b}", align_bytes=64) for b in range(3)]
+        key_scale = [keep.tile([P, I], U8, name=f"key_scale{b}", align_bytes=64) for b in range(BOOKS)]
         nc.vector.tensor_copy(key[0][:].bitcast(U16), key_tab[0][:].bitcast(U16).indirect(lists[0][:]))
         for b in (1, 2):
             nc.vector.tensor_copy(key[b][:], key_tab[b][:].bitcast(U32).indirect(lists[b][:]))
+        q_bf = keep.tile([P, Q, PACK], BF16, name="q_bf", align_bytes=64)
+        nc.vector.tensor_copy(q_bf[:].rearrange("p (c i) t -> p c t i", i=4),
+                              q_raw[:].rearrange("p t (c i) -> p c t i", i=4))
+        q_codes = keep.tile([P, Q], U32, name="q_codes", align_bytes=64)
+        q_scales = keep.tile([P, Q], U8, name="q_scales", align_bytes=64)
         score = [psum.tile([P, I], F32, name=f"score{h}", tag=f"score{h}") for h in range(HALVES)]
-        for b in range(3):
+        for b in range(BOOKS):
             nc.vector.tensor_copy(key_scale[b][:], scale_tab[b][:].indirect(lists[b][:]))
+            if b == 0:
+                nc.vector.quantize_mx(out=q_codes[:].bitcast(FP8X4), scales=q_scales[:],
+                                      in_=q_bf[:].rearrange("p q t -> p (q t)"))
             for h in range(HALVES):
                 cols = slice(P * h, P * (h + 1))
                 nc.tensor.matmul_mx(out=score[h][:], lhsT=q_codes[:, cols].bitcast(FP8X4), lhsT_scale=q_scales[:, cols],
                                     rhs=key[b][:].bitcast(FP4X4 if b == 0 else FP8X4), rhs_scale=key_scale[b][:],
-                                    start=(b == 0), stop=(b == 2))
+                                    start=(b == 0), stop=(b == BOOKS - 1))
 
-        neg_max = keep.tile([P, HALVES], F32, name="neg_max", tag="neg_max")
-        row_sum = keep.tile([P, HALVES], F32, name="row_sum")
+        summed = [psum.tile([P, PACK, P], F32, name=f"summed{j}", tag=f"sum{j}") for j in range(PACK)]
+
+        order = places[:6] + [(2, 0), (2, 2), (2, 1)] + places[9:]
+
+        def gather_and_turn(j, b):
+            picked = keep.tile([P, I], F32, name=f"picked{j}{b}", tag=FOLLOWS.get((j, b), f"picked{j}{b}"))
+            if (j, b) in ON_VECTOR:
+                nc.vector.tensor_copy(picked[:].bitcast(U32).rearrange("p (t s) -> p s t", t=PACK),
+                                      val_tab[j, b][:].bitcast(U32).indirect(lists[b][:]))
+                planes = [picked[:, P * t:P * (t + 1)] for t in range(PACK)]
+            else:
+                nc.scalar.activation(picked[:], val_tab[j, b][:].indirect(lists[b][:]), ACT.Copy)
+                planes = [picked[:, t:I:PACK] for t in range(PACK)]
+            for t in range(PACK):
+                nc.tensor.matmul(summed[j][:, t, :], lhsT=planes[t], rhs=ident[:], is_transpose=True,
+                                 start=((j, b) == order[BOOKS * j] and t == 0),
+                                 stop=((j, b) == order[BOOKS * j + BOOKS - 1] and t == PACK - 1))
+
+        woven = keep.tile([P, Q + 2 * P, PACK], BF16, name="woven", tag="early", align_bytes=64)
+
+        def scale_values(j, v_bf):
+            nc.vector.tensor_tensor(v_bf, summed[j][:].rearrange("p t m -> p m t"),
+                                    vsc_t[:].unsqueeze(1).to_broadcast([P, P, PACK]), ALU.mult)
+
+        for place in order[:6]:
+            gather_and_turn(*place)
+        scale_values(0, woven[:, Q:Q + P, :])
+        for place in order[6:9]:
+            gather_and_turn(*place)
+
+        size_row = psum.tile([P, PACK, P], F32, name="size_row", tag="size")
+        for t in range(PACK):
+            nc.tensor.transpose(size_row[:, t, :], size_t[:, t:t + 1].to_broadcast([P, P]), ident[:])
+        neg_max = keep.tile([P, HALVES], F32, name="neg_max")
+        row_sum = keep.tile([P, HALVES], F32, name="row_sum", tag="row_sum", align_bytes=64)
         inv_sum = keep.tile([P, HALVES], F32, name="inv_sum")
-        prob = [keep.tile([P, PACK, P], F32, name=f"prob{h}") for h in range(HALVES)]
+        prob = [keep.tile([P, I], F32, name=f"prob{h}", tag=("val_tab12", "prob1")[h])[:] for h in range(HALVES)]
         for h in range(HALVES):
             nc.vector.tensor_reduce(neg_max[:, h:h + 1], score[h][:], AXIS.X, ALU.max, negate=True)
-            nc.scalar.activation(prob[h][:], score[h][:].rearrange("p (s t) -> p t s", t=PACK), ACT.Exp,
+            nc.scalar.activation(prob[h], score[h][:], ACT.Exp,
                                  bias=neg_max[:, h:h + 1], accum_out=row_sum[:, h:h + 1])
+        scale_values(1, woven[:, Q + P:Q + 2 * P, :])
         nc.vector.reciprocal(inv_sum[:], row_sum[:])
-        w_planes = keep.tile([P, PACK, Q], BF16, name="w_planes")
-        early_bf = keep.tile([P, Q + 3 * P, PACK], BF16, name="early_bf", tag="early", align_bytes=64)
+        w_turned = psum.tile([P, HALVES, 2, P], F32, name="w_turned", tag="w")
+        for h in range(HALVES):
+            w_bf = keep.tile([P, I], BF16, name=f"w_bf{h}")
+            nc.vector.scalar_tensor_tensor(w_bf[:].rearrange("p (s t) -> p s t", t=PACK),
+                                           prob[h].rearrange("p (s t) -> p s t", t=PACK), inv_sum[:, h:h + 1],
+                                           size_row[:].rearrange("p t s -> p s t"), ALU.mult, ALU.mult)
+            for u in range(2):
+                nc.tensor.transpose(w_turned[:, h, u, :], w_bf[:].bitcast(F32)[:, u:I // 2:2], ident[:])
+        nc.scalar.copy(woven[:, :Q, :].rearrange("p q t -> p (q t)").bitcast(F32).rearrange("p (h q u) -> p h q u", h=HALVES, u=2),
+                       w_turned[:].rearrange("p h u q -> p h q u"))
+        third_bf = keep.tile([P, P, PACK], BF16, name="third_bf", tag="row_sum", align_bytes=64)
+        scale_values(2, third_bf[:])
+        for place in places[9:]:
+            gather_and_turn(*place)
+
         early_codes = keep.tile([P, Q + 2 * P], U32, name="early_codes", align_bytes=64)
         early_scales = keep.tile([P, Q + 2 * P], U8, name="early_scales", align_bytes=64)
-        w_turned = [psum.tile([P, 2, Q], F32, name=f"w_turned{u}", tag=f"acc{u}") for u in range(2)]
-        for h in range(HALVES):
-            normed = keep.tile([P, PACK, P], F32, name=f"normed{h}")
-            nc.scalar.activation(normed[:], prob[h][:], ACT.Copy, scale=inv_sum[:, h:h + 1])
-            for t in range(PACK):
-                nc.tensor.transpose(w_turned[t // 2][:, t % 2, P * h:P * (h + 1)], normed[:, t, :], ident[:])
-        for t in range(PACK):
-            nc.scalar.activation(w_planes[:, t, :], w_turned[t // 2][:, t % 2, :], ACT.Copy, scale=size_t[:, t:t + 1])
-        nc.scalar.copy(early_bf[:, :Q, :].rearrange("p (c i) t -> p c t i", i=4),
-                       w_planes[:].rearrange("p t (c i) -> p c t i", i=4))
-
-        acc_early = [psum.tile([P, 2, P], F32, name=f"acc_early{h}", tag=f"acc{h}") for h in range(HALVES)]
-        acc = [psum.tile([P, 2, P], F32, name=f"acc_late{h}", tag=f"score{h}") for h in range(HALVES)]
+        acc_early = [psum.tile([P, 2, P], F32, name=f"acc_early{h}", tag=f"score{h}") for h in range(HALVES)]
+        acc = [psum.tile([P, 2, P], F32, name=f"acc_late{h}", tag=("size", "w")[h]) for h in range(HALVES)]
         o_sb = keep.tile([P, PACK, Q], F32, name="o_sb")
         o_rows = out_0.rearrange("(p t) q -> p t q", t=PACK)
         o_bf = keep.tile([P, Q, PACK], BF16, name="o_bf", tag="vsc", align_bytes=64)
-
-        def gather_and_turn(j, picked):
-            if j == 2:
-                first = psum.tile([P, P], F32, name="summed2_first", tag="turn0")
-                others = psum.tile([P, PACK - 1, P], F32, name="summed2_others", tag="turn2")
-                summed, opens, closes = [first[:]] + [others[:, t, :] for t in range(PACK - 1)], (0, 1), (0, PACK - 1)
-            else:
-                whole = psum.tile([P, PACK, P], F32, name=f"summed{j}", tag=f"turn{min(j, 2)}")
-                summed, opens, closes = [whole[:, t, :] for t in range(PACK)], (0,), (PACK - 1,)
-            for b in range(3):
-                window = val_tab[b][j // 2][:, START[j]:START[j] + WIN]
-                nc.vector.tensor_copy(picked[b].bitcast(U32).rearrange("p t s -> p s t"),
-                                      window.bitcast(U32).indirect(lists[b][:]))
-                for t in range(PACK):
-                    nc.tensor.matmul(summed[t], lhsT=picked[b][:, t, :], rhs=ident[:], is_transpose=True,
-                                     start=(b == 0 and t in opens), stop=(b == 2 and t in closes))
-            return whole if j == PACK - 1 else summed
-
-        def scale_on_scalar(j, summed, v_bf):
-            v_planes = keep.tile([P, PACK, P], BF16, name=f"v_planes{j}")
-            for t in range(PACK):
-                nc.scalar.activation(v_planes[:, t, :], summed[t], ACT.Copy, scale=vsc_t[:, t:t + 1])
-            nc.scalar.copy(v_bf.rearrange("p (c i) t -> p c t i", i=4),
-                           v_planes[:].rearrange("p t (c i) -> p c t i", i=4))
 
         def product(j, v_codes, v_scales):
             for h in range(HALVES):
@@ -176,23 +209,8 @@ def tile_attend_additivekeys_pl_kernel(tc, query, ba_words, ba_scales, bb_words,
             queue = nc.sync if u == 0 else nc.scalar
             queue.dma_start(o_rows[:, 2 * u:2 * u + 2, :], o_sb[:, 2 * u:2 * u + 2, :])
 
-        picked = {place: keep.tile([P, PACK, P], F32, name=f"picked{place[0]}{place[1]}")[:]
-                  for place in ((0, 0), (0, 1), (0, 2))}
-        picked[1, 0] = keep.tile([P, PACK, P], F32, name="picked10", tag="key_scale2", align_bytes=64)[:]
-        rest = [(j, b) for j in range(PACK) for b in range(3) if (j, b) not in picked]
-        picked_rest = keep.tile([P, len(rest), PACK, P], F32, name="picked_rest", tag="neg_max")
-        for n, place in enumerate(rest):
-            picked[place] = picked_rest[:, n]
-        for j in range(3):
-            summed = gather_and_turn(j, [picked[j, b] for b in range(3)])
-            scale_on_scalar(j, summed, early_bf[:, Q + P * j:Q + P * (j + 1), :])
-        warm = psum.tile([P, I], F32, name="warm", tag="turn0")
-        for n in range(2):
-            nc.tensor.matmul_mx(out=warm[:], lhsT=q_codes[:, :P].bitcast(FP8X4), lhsT_scale=q_scales[:, :P],
-                                rhs=key[1][:].bitcast(FP8X4), rhs_scale=key_scale[1][:], start=(n == 0), stop=(n == 1))
-        summed3 = gather_and_turn(3, [picked[3, b] for b in range(3)])
         nc.vector.quantize_mx(out=early_codes[:].bitcast(FP8X4), scales=early_scales[:],
-                              in_=early_bf[:, :Q + 2 * P, :].rearrange("p m t -> p (m t)"))
+                              in_=woven[:].rearrange("p m t -> p (m t)"))
         for h in range(HALVES):
             rows = slice(P * h, P * (h + 1))
             for j in range(2):
@@ -205,11 +223,10 @@ def tile_attend_additivekeys_pl_kernel(tc, query, ba_words, ba_scales, bb_words,
         late_codes = [keep.tile([P, P], U32, name=f"late_codes{j}", align_bytes=64) for j in range(2)]
         late_scales = [keep.tile([P, P], U8, name=f"late_scales{j}", align_bytes=64) for j in range(2)]
         nc.vector.quantize_mx(out=late_codes[0][:].bitcast(FP8X4), scales=late_scales[0][:],
-                              in_=early_bf[:, Q + 2 * P:, :].rearrange("p m t -> p (m t)"))
+                              in_=third_bf[:].rearrange("p m t -> p (m t)"))
         product(2, late_codes[0][:], late_scales[0][:])
         last_bf = keep.tile([P, P, PACK], BF16, name="last_bf", tag="early", align_bytes=64)
-        nc.vector.tensor_tensor(last_bf[:], summed3[:].rearrange("p t m -> p m t"),
-                                vsc_t[:].unsqueeze(1).to_broadcast([P, P, PACK]), ALU.mult)
+        scale_values(3, last_bf[:])
         nc.vector.quantize_mx(out=late_codes[1][:].bitcast(FP8X4), scales=late_scales[1][:],
                               in_=last_bf[:].rearrange("p m t -> p (m t)"))
         product(3, late_codes[1][:], late_scales[1][:])

@@ -26,7 +26,6 @@ WIN16 = 1024
 WIN_SCALAR = U + 8
 HALVES = Q // P
 ON_VECTOR = ((2, 2), (3, 2))
-FOLLOWS = {(3, 1): "val_tab12", (3, 2): "prob1"}
 
 
 def tile_attend_additivekeys_pl_kernel(tc, query, ba_words, ba_scales, bb_words, bb_scales, bc_words, bc_scales,
@@ -57,11 +56,12 @@ def tile_attend_additivekeys_pl_kernel(tc, query, ba_words, ba_scales, bb_words,
             nc.vector.memset(key_tab[b][:, U:], 0)
         nc.gpsimd.memset(val_tab[places[0]][:, U:], 0.0)
         make_identity(nc, ident[:])
+        size_t = keep.tile([P, PACK], F32, name="size_t")
+        nc.gpsimd.dma_start(size_t[:], size.rearrange("o (p t) -> (o p) t", t=PACK))
         for place in places[1:]:
             nc.gpsimd.memset(val_tab[place][:, U:], 0.0)
 
         q_raw = keep.tile([P, PACK, Q], F32, name="q_raw")
-        size_t = keep.tile([P, PACK], F32, name="size_t")
         vsc_t = keep.tile([P, PACK], F32, name="vsc_t", tag="vsc", align_bytes=64)
         val_rows = [table.rearrange("(p t) u -> p (t u)", t=PACK) for table in (ca, cb, cc)]
 
@@ -90,13 +90,12 @@ def tile_attend_additivekeys_pl_kernel(tc, query, ba_words, ba_scales, bb_words,
         load_values(1, 0)
         load_scales(1, bb_scales)
         load_values(1, 1)
-        nc.sync.dma_start(vsc_t[:], vsc.rearrange("(p t) o -> p (t o)", t=PACK))
-        nc.sync.dma_start(size_t[:], size.rearrange("o (p t) -> (o p) t", t=PACK))
+        load_values(1, 2)
         load_values(2, 0)
         load_scales(2, bc_scales)
         load_values(2, 2)
-        load_values(1, 2)
         load_values(2, 1)
+        nc.sync.dma_start(vsc_t[:], vsc.rearrange("(p t) o -> p (t o)", t=PACK))
         for place in places[9:]:
             load_values(*place)
 
@@ -124,23 +123,28 @@ def tile_attend_additivekeys_pl_kernel(tc, query, ba_words, ba_scales, bb_words,
                                     rhs=key[b][:].bitcast(FP4X4 if b == 0 else FP8X4), rhs_scale=key_scale[b][:],
                                     start=(b == 0), stop=(b == BOOKS - 1))
 
-        summed = [psum.tile([P, PACK, P], F32, name=f"summed{j}", tag=f"sum{j}") for j in range(PACK)]
+        summed = [psum.tile([P, PACK, P], F32, name=f"summed{j}", tag=f"sum{j}") for j in range(PACK - 1)]
 
-        order = places[:6] + [(2, 0), (2, 2), (2, 1)] + places[9:]
+        picked = {}
 
-        def gather_and_turn(j, b):
-            picked = keep.tile([P, I], F32, name=f"picked{j}{b}", tag=FOLLOWS.get((j, b), f"picked{j}{b}"))
+        def gather(j, b, tag=None):
+            picked[j, b] = keep.tile([P, I], F32, name=f"picked{j}{b}", tag=tag or f"picked{j}{b}")
             if (j, b) in ON_VECTOR:
-                nc.vector.tensor_copy(picked[:].bitcast(U32).rearrange("p (t s) -> p s t", t=PACK),
+                nc.vector.tensor_copy(picked[j, b][:].bitcast(U32).rearrange("p (t s) -> p s t", t=PACK),
                                       val_tab[j, b][:].bitcast(U32).indirect(lists[b][:]))
-                planes = [picked[:, P * t:P * (t + 1)] for t in range(PACK)]
             else:
-                nc.scalar.activation(picked[:], val_tab[j, b][:].indirect(lists[b][:]), ACT.Copy)
-                planes = [picked[:, t:I:PACK] for t in range(PACK)]
+                nc.scalar.activation(picked[j, b][:], val_tab[j, b][:].indirect(lists[b][:]), ACT.Copy)
+
+        def add(name, left, right, tag=None):
+            both = keep.tile([P, I], F32, name=name, tag=tag or name, align_bytes=64)
+            nc.gpsimd.tensor_tensor(both[:], left[:], right[:], ALU.add)
+            return both
+
+        def turn(j, tile, dealt, opens, closes):
             for t in range(PACK):
-                nc.tensor.matmul(summed[j][:, t, :], lhsT=planes[t], rhs=ident[:], is_transpose=True,
-                                 start=((j, b) == order[BOOKS * j] and t == 0),
-                                 stop=((j, b) == order[BOOKS * j + BOOKS - 1] and t == PACK - 1))
+                plane = tile[:, P * t:P * (t + 1)] if dealt else tile[:, t:I:PACK]
+                nc.tensor.matmul(summed[j][:, t, :], lhsT=plane, rhs=ident[:], is_transpose=True,
+                                 start=(opens and t == 0), stop=(closes and t == PACK - 1))
 
         woven = keep.tile([P, Q + 2 * P, PACK], BF16, name="woven", tag="early", align_bytes=64)
 
@@ -148,11 +152,14 @@ def tile_attend_additivekeys_pl_kernel(tc, query, ba_words, ba_scales, bb_words,
             nc.vector.tensor_tensor(v_bf, summed[j][:].rearrange("p t m -> p m t"),
                                     vsc_t[:].unsqueeze(1).to_broadcast([P, P, PACK]), ALU.mult)
 
-        for place in order[:6]:
-            gather_and_turn(*place)
-        scale_values(0, woven[:, Q:Q + P, :])
-        for place in order[6:9]:
-            gather_and_turn(*place)
+        for place in places[:9]:
+            gather(*place)
+        for b in range(BOOKS):
+            turn(0, picked[0, b], False, b == 0, b == BOOKS - 1)
+        pair1 = add("pair1", picked[1, 0], picked[1, 1])
+        turn(2, picked[2, 2], True, True, False)
+        turn(1, add("triple1", pair1, picked[1, 2], "scale_tab2"), False, True, True)
+        turn(2, add("pair2", picked[2, 0], picked[2, 1]), False, False, True)
 
         size_row = psum.tile([P, PACK, P], F32, name="size_row", tag="size")
         for t in range(PACK):
@@ -160,12 +167,13 @@ def tile_attend_additivekeys_pl_kernel(tc, query, ba_words, ba_scales, bb_words,
         neg_max = keep.tile([P, HALVES], F32, name="neg_max")
         row_sum = keep.tile([P, HALVES], F32, name="row_sum", tag="row_sum", align_bytes=64)
         inv_sum = keep.tile([P, HALVES], F32, name="inv_sum")
-        prob = [keep.tile([P, I], F32, name=f"prob{h}", tag=("val_tab12", "prob1")[h])[:] for h in range(HALVES)]
+        prob = [keep.tile([P, I], F32, name=f"prob{h}", tag=f"prob{h}")[:] for h in range(HALVES)]
         for h in range(HALVES):
             nc.vector.tensor_reduce(neg_max[:, h:h + 1], score[h][:], AXIS.X, ALU.max, negate=True)
             nc.scalar.activation(prob[h], score[h][:], ACT.Exp,
                                  bias=neg_max[:, h:h + 1], accum_out=row_sum[:, h:h + 1])
-        scale_values(1, woven[:, Q + P:Q + 2 * P, :])
+        for j in range(2):
+            scale_values(j, woven[:, Q + P * j:Q + P * (j + 1), :])
         nc.vector.reciprocal(inv_sum[:], row_sum[:])
         w_turned = psum.tile([P, HALVES, 2, P], F32, name="w_turned", tag="w")
         for h in range(HALVES):
@@ -179,13 +187,15 @@ def tile_attend_additivekeys_pl_kernel(tc, query, ba_words, ba_scales, bb_words,
                        w_turned[:].rearrange("p h u q -> p h q u"))
         third_bf = keep.tile([P, P, PACK], BF16, name="third_bf", tag="row_sum", align_bytes=64)
         scale_values(2, third_bf[:])
-        for place in places[9:]:
-            gather_and_turn(*place)
+        summed.append(psum.tile([P, PACK, P], F32, name="summed3", tag="size"))
+        for b, tag in enumerate((None, None, "prob1")):
+            gather(3, b, tag)
+            turn(3, picked[3, b], b == 2, b == 0, b == 2)
 
         early_codes = keep.tile([P, Q + 2 * P], U32, name="early_codes", align_bytes=64)
         early_scales = keep.tile([P, Q + 2 * P], U8, name="early_scales", align_bytes=64)
         acc_early = [psum.tile([P, 2, P], F32, name=f"acc_early{h}", tag=f"score{h}") for h in range(HALVES)]
-        acc = [psum.tile([P, 2, P], F32, name=f"acc_late{h}", tag=("size", "w")[h]) for h in range(HALVES)]
+        acc = [psum.tile([P, 2, P], F32, name=f"acc_late{h}", tag=("sum0", "w")[h]) for h in range(HALVES)]
         o_sb = keep.tile([P, PACK, Q], F32, name="o_sb")
         o_rows = out_0.rearrange("(p t) q -> p t q", t=PACK)
         o_bf = keep.tile([P, Q, PACK], BF16, name="o_bf", tag="vsc", align_bytes=64)

@@ -95,9 +95,10 @@ def tile_attend_additivekeys_pl_kernel(tc, query, ba_words, ba_scales, bb_words,
         load_scales(2, bc_scales)
         load_values(2, 2)
         load_values(2, 1)
+        load_values(3, 2)
         nc.sync.dma_start(vsc_t[:], vsc.rearrange("(p t) o -> p (t o)", t=PACK))
-        for place in places[9:]:
-            load_values(*place)
+        load_values(3, 0)
+        load_values(3, 1)
 
         key = [keep.tile([P, 2 * I], U8, name="key0", align_bytes=64),
                keep.tile([P, I], U32, name="key1", align_bytes=64),
@@ -123,7 +124,7 @@ def tile_attend_additivekeys_pl_kernel(tc, query, ba_words, ba_scales, bb_words,
                                     rhs=key[b][:].bitcast(FP4X4 if b == 0 else FP8X4), rhs_scale=key_scale[b][:],
                                     start=(b == 0), stop=(b == BOOKS - 1))
 
-        summed = [psum.tile([P, PACK, P], F32, name=f"summed{j}", tag=f"sum{j}") for j in range(PACK - 1)]
+        summed = [psum.tile([P, PACK, P], F32, name=f"summed{j}", tag=f"sum{j}") for j in range(PACK)]
 
         picked = {}
 
@@ -146,8 +147,6 @@ def tile_attend_additivekeys_pl_kernel(tc, query, ba_words, ba_scales, bb_words,
                 nc.tensor.matmul(summed[j][:, t, :], lhsT=plane, rhs=ident[:], is_transpose=True,
                                  start=(opens and t == 0), stop=(closes and t == PACK - 1))
 
-        woven = keep.tile([P, Q + 2 * P, PACK], BF16, name="woven", tag="early", align_bytes=64)
-
         def scale_values(j, v_bf):
             nc.vector.tensor_tensor(v_bf, summed[j][:].rearrange("p t m -> p m t"),
                                     vsc_t[:].unsqueeze(1).to_broadcast([P, P, PACK]), ALU.mult)
@@ -166,15 +165,17 @@ def tile_attend_additivekeys_pl_kernel(tc, query, ba_words, ba_scales, bb_words,
             nc.tensor.transpose(size_row[:, t, :], size_t[:, t:t + 1].to_broadcast([P, P]), ident[:])
         neg_max = keep.tile([P, HALVES], F32, name="neg_max")
         row_sum = keep.tile([P, HALVES], F32, name="row_sum", tag="row_sum", align_bytes=64)
-        inv_sum = keep.tile([P, HALVES], F32, name="inv_sum")
-        prob = [keep.tile([P, I], F32, name=f"prob{h}", tag=f"prob{h}")[:] for h in range(HALVES)]
+        inv_sum = keep.tile([P, HALVES], F32, name="inv_sum", tag="inv_sum", align_bytes=64)
+        shared = keep.tile([P, I + I // 2], F32, name="shared")
+        prob = [keep.tile([P, I], F32, name="prob0")[:], shared[:, I // 2:]]
         for h in range(HALVES):
             nc.vector.tensor_reduce(neg_max[:, h:h + 1], score[h][:], AXIS.X, ALU.max, negate=True)
             nc.scalar.activation(prob[h], score[h][:], ACT.Exp,
                                  bias=neg_max[:, h:h + 1], accum_out=row_sum[:, h:h + 1])
-        for j in range(2):
-            scale_values(j, woven[:, Q + P * j:Q + P * (j + 1), :])
+        gather(3, 2)
+        turn(3, picked[3, 2], True, True, False)
         nc.vector.reciprocal(inv_sum[:], row_sum[:])
+        woven = keep.tile([P, Q + 2 * P, PACK], BF16, name="woven", tag="row_sum", align_bytes=64)
         w_turned = psum.tile([P, HALVES, 2, P], F32, name="w_turned", tag="w")
         for h in range(HALVES):
             w_bf = keep.tile([P, I], BF16, name=f"w_bf{h}")
@@ -183,19 +184,23 @@ def tile_attend_additivekeys_pl_kernel(tc, query, ba_words, ba_scales, bb_words,
                                            size_row[:].rearrange("p t s -> p s t"), ALU.mult, ALU.mult)
             for u in range(2):
                 nc.tensor.transpose(w_turned[:, h, u, :], w_bf[:].bitcast(F32)[:, u:I // 2:2], ident[:])
+        gather(3, 0)
+        turn(3, picked[3, 0], False, False, False)
+        for half in range(2):
+            nc.scalar.activation(shared[:, I // 2 * half:I // 2 * (half + 1)],
+                                 val_tab[3, 1][:].indirect(lists[1][:, 16 * half:16 * (half + 1)]), ACT.Copy)
+        turn(3, shared, False, False, True)
         nc.scalar.copy(woven[:, :Q, :].rearrange("p q t -> p (q t)").bitcast(F32).rearrange("p (h q u) -> p h q u", h=HALVES, u=2),
                        w_turned[:].rearrange("p h u q -> p h q u"))
-        third_bf = keep.tile([P, P, PACK], BF16, name="third_bf", tag="row_sum", align_bytes=64)
+        for j in range(2):
+            scale_values(j, woven[:, Q + P * j:Q + P * (j + 1), :])
+        third_bf = keep.tile([P, P, PACK], BF16, name="third_bf", tag="inv_sum", align_bytes=64)
         scale_values(2, third_bf[:])
-        summed.append(psum.tile([P, PACK, P], F32, name="summed3", tag="size"))
-        for b, tag in enumerate((None, None, "prob1")):
-            gather(3, b, tag)
-            turn(3, picked[3, b], b == 2, b == 0, b == 2)
 
         early_codes = keep.tile([P, Q + 2 * P], U32, name="early_codes", align_bytes=64)
         early_scales = keep.tile([P, Q + 2 * P], U8, name="early_scales", align_bytes=64)
         acc_early = [psum.tile([P, 2, P], F32, name=f"acc_early{h}", tag=f"score{h}") for h in range(HALVES)]
-        acc = [psum.tile([P, 2, P], F32, name=f"acc_late{h}", tag=("sum0", "w")[h]) for h in range(HALVES)]
+        acc = [psum.tile([P, 2, P], F32, name=f"acc_late{h}", tag=("size", "w")[h]) for h in range(HALVES)]
         o_sb = keep.tile([P, PACK, Q], F32, name="o_sb")
         o_rows = out_0.rearrange("(p t) q -> p t q", t=PACK)
         o_bf = keep.tile([P, Q, PACK], BF16, name="o_bf", tag="vsc", align_bytes=64)
@@ -232,11 +237,11 @@ def tile_attend_additivekeys_pl_kernel(tc, query, ba_words, ba_scales, bb_words,
         store(0)
         late_codes = [keep.tile([P, P], U32, name=f"late_codes{j}", align_bytes=64) for j in range(2)]
         late_scales = [keep.tile([P, P], U8, name=f"late_scales{j}", align_bytes=64) for j in range(2)]
+        last_bf = keep.tile([P, P, PACK], BF16, name="last_bf", align_bytes=64)
+        scale_values(3, last_bf[:])
         nc.vector.quantize_mx(out=late_codes[0][:].bitcast(FP8X4), scales=late_scales[0][:],
                               in_=third_bf[:].rearrange("p m t -> p (m t)"))
         product(2, late_codes[0][:], late_scales[0][:])
-        last_bf = keep.tile([P, P, PACK], BF16, name="last_bf", tag="early", align_bytes=64)
-        scale_values(3, last_bf[:])
         nc.vector.quantize_mx(out=late_codes[1][:].bitcast(FP8X4), scales=late_scales[1][:],
                               in_=last_bf[:].rearrange("p m t -> p (m t)"))
         product(3, late_codes[1][:], late_scales[1][:])

@@ -175,7 +175,8 @@ def tile_attend_additivekeys_pl_kernel(tc, query, ba_words, ba_scales, bb_words,
         gather(3, 2)
         turn(3, picked[3, 2], True, True, False)
         nc.vector.reciprocal(inv_sum[:], row_sum[:])
-        woven = keep.tile([P, Q + 2 * P, PACK], BF16, name="woven", tag="row_sum", align_bytes=64)
+        w_woven = keep.tile([P, Q, PACK], BF16, name="w_woven", align_bytes=64)
+        v_woven = keep.tile([P, 2 * P, PACK], BF16, name="v_woven", tag="row_sum", align_bytes=64)
         w_turned = psum.tile([P, HALVES, 2, P], F32, name="w_turned", tag="w")
         for h in range(HALVES):
             w_bf = keep.tile([P, I], BF16, name=f"w_bf{h}")
@@ -190,15 +191,17 @@ def tile_attend_additivekeys_pl_kernel(tc, query, ba_words, ba_scales, bb_words,
             nc.scalar.activation(shared[:, I // 2 * half:I // 2 * (half + 1)],
                                  val_tab[3, 1][:].indirect(lists[1][:, 16 * half:16 * (half + 1)]), ACT.Copy)
         turn(3, shared, False, False, True)
-        nc.scalar.copy(woven[:, :Q, :].rearrange("p q t -> p (q t)").bitcast(F32).rearrange("p (h q u) -> p h q u", h=HALVES, u=2),
+        nc.scalar.copy(w_woven[:].rearrange("p q t -> p (q t)").bitcast(F32).rearrange("p (h q u) -> p h q u", h=HALVES, u=2),
                        w_turned[:].rearrange("p h u q -> p h q u"))
         for j in range(2):
-            scale_values(j, woven[:, Q + P * j:Q + P * (j + 1), :])
+            scale_values(j, v_woven[:, P * j:P * (j + 1), :])
         third_bf = keep.tile([P, P, PACK], BF16, name="third_bf", tag="inv_sum", align_bytes=64)
         scale_values(2, third_bf[:])
 
-        early_codes = keep.tile([P, Q + 2 * P], U32, name="early_codes", align_bytes=64)
-        early_scales = keep.tile([P, Q + 2 * P], U8, name="early_scales", align_bytes=64)
+        early_codes = keep.tile([P, 2 * P], U32, name="early_codes", align_bytes=64)
+        early_scales = keep.tile([P, 2 * P], U8, name="early_scales", align_bytes=64)
+        w_codes = keep.tile([P, Q], U32, name="w_codes", align_bytes=64)
+        w_scales = keep.tile([P, Q], U8, name="w_scales", align_bytes=64)
         acc_early = [psum.tile([P, 2, P], F32, name=f"acc_early{h}", tag=f"score{h}") for h in range(HALVES)]
         acc = [psum.tile([P, 2, P], F32, name=f"acc_late{h}", tag=("size", "w")[h]) for h in range(HALVES)]
         o_sb = keep.tile([P, PACK, Q], F32, name="o_sb")
@@ -209,7 +212,7 @@ def tile_attend_additivekeys_pl_kernel(tc, query, ba_words, ba_scales, bb_words,
             for h in range(HALVES):
                 cols = slice(P * h, P * (h + 1))
                 nc.tensor.matmul_mx(out=acc[h][:, j % 2, :], lhsT=v_codes.bitcast(FP8X4), lhsT_scale=v_scales,
-                                    rhs=early_codes[:, cols].bitcast(FP8X4), rhs_scale=early_scales[:, cols],
+                                    rhs=w_codes[:, cols].bitcast(FP8X4), rhs_scale=w_scales[:, cols],
                                     start=True, stop=True)
 
         def unload(h):
@@ -225,14 +228,16 @@ def tile_attend_additivekeys_pl_kernel(tc, query, ba_words, ba_scales, bb_words,
             queue.dma_start(o_rows[:, 2 * u:2 * u + 2, :], o_sb[:, 2 * u:2 * u + 2, :])
 
         nc.vector.quantize_mx(out=early_codes[:].bitcast(FP8X4), scales=early_scales[:],
-                              in_=woven[:].rearrange("p m t -> p (m t)"))
+                              in_=v_woven[:].rearrange("p m t -> p (m t)"))
+        nc.vector.quantize_mx(out=w_codes[:].bitcast(FP8X4), scales=w_scales[:],
+                              in_=w_woven[:].rearrange("p m t -> p (m t)"))
         for h in range(HALVES):
             rows = slice(P * h, P * (h + 1))
             for j in range(2):
-                cols = slice(Q + P * j, Q + P * (j + 1))
+                cols = slice(P * j, P * (j + 1))
                 nc.tensor.matmul_mx(out=acc_early[h][:, j, :], lhsT=early_codes[:, cols].bitcast(FP8X4),
-                                    lhsT_scale=early_scales[:, cols], rhs=early_codes[:, rows].bitcast(FP8X4),
-                                    rhs_scale=early_scales[:, rows], start=True, stop=True)
+                                    lhsT_scale=early_scales[:, cols], rhs=w_codes[:, rows].bitcast(FP8X4),
+                                    rhs_scale=w_scales[:, rows], start=True, stop=True)
             nc.scalar.copy(o_sb[:, :2, rows], acc_early[h][:])
         store(0)
         late_codes = [keep.tile([P, P], U32, name=f"late_codes{j}", align_bytes=64) for j in range(2)]

@@ -71,8 +71,8 @@ def tile_attend_additivekeys_pl_kernel(tc, query, ba_words, ba_scales, bb_words,
         def load_keys(b, words):
             nc.sync.dma_start(key_tab[b][:, :U], words[0].rearrange("p n t -> p (n t)").bitcast(I32))
 
-        def load_scales(b, scales):
-            for quad in range(4):
+        def load_scale_rows(b, scales, quads):
+            for quad in quads:
                 nc.sync.dma_start(scale_tab[b][32 * quad:32 * quad + 4, :U].bitcast(I32),
                                   scales[0, 4 * quad:4 * quad + 4, :].bitcast(I32))
 
@@ -81,21 +81,22 @@ def tile_attend_additivekeys_pl_kernel(tc, query, ba_words, ba_scales, bb_words,
         load_values(0, 0)
         nc.sync.dma_start(lists[1][:], offs2)
         load_keys(1, bb_words)
+        load_scale_rows(0, ba_scales, (0,))
         load_values(0, 1)
+        load_scale_rows(0, ba_scales, (1,))
         load_keys(2, bc_words)
         nc.sync.dma_start(lists[2][:], offs3)
-        load_scales(0, ba_scales)
         load_values(0, 2)
+        load_scale_rows(0, ba_scales, (2, 3))
         nc.sync.dma_start(q_raw[:], query.rearrange("(p t) q -> p t q", t=PACK))
+        load_scale_rows(1, bb_scales, (0,))
         load_values(1, 0)
-        load_scales(1, bb_scales)
-        load_values(1, 1)
-        load_values(1, 2)
-        load_values(2, 0)
-        load_scales(2, bc_scales)
-        load_values(2, 2)
-        load_values(2, 1)
-        load_values(3, 2)
+        load_scale_rows(1, bb_scales, (1, 2, 3))
+        for place in ((1, 1), (1, 2), (2, 0)):
+            load_values(*place)
+        load_scale_rows(2, bc_scales, range(4))
+        for place in ((2, 2), (2, 1), (3, 2)):
+            load_values(*place)
         nc.sync.dma_start(vsc_t[:], vsc.rearrange("(p t) o -> p (t o)", t=PACK))
         load_values(3, 0)
         load_values(3, 1)

@@ -152,8 +152,11 @@ def tile_attend_additivekeys_pl_kernel(tc, query, ba_words, ba_scales, bb_words,
             nc.vector.tensor_tensor(v_bf, summed[j][:].rearrange("p t m -> p m t"),
                                     vsc_t[:].unsqueeze(1).to_broadcast([P, P, PACK]), ALU.mult)
 
-        for place in places[:9]:
+        for place in places[:7] + places[8:9]:
             gather(*place)
+        picked[2, 1] = keep.tile([P, I], F32, name="picked21")
+        nc.scalar.activation(picked[2, 1][:, :I // 2], val_tab[2, 1][:].indirect(lists[1][:, :16]), ACT.Copy)
+        nc.vector.tensor_copy(picked[2, 1][:, I // 2:], val_tab[2, 1][:].indirect(lists[1][:, 16:]))
         for b in range(BOOKS):
             turn(0, picked[0, b], False, b == 0, b == BOOKS - 1)
         pair1 = add("pair1", picked[1, 0], picked[1, 1])

@@ -157,8 +157,8 @@ def tile_attend_additivekeys_pl_kernel(tc, query, ba_words, ba_scales, bb_words,
         picked[2, 1] = keep.tile([P, I], F32, name="picked21")
         nc.scalar.activation(picked[2, 1][:, :I // 2], val_tab[2, 1][:].indirect(lists[1][:, :16]), ACT.Copy)
         nc.vector.tensor_copy(picked[2, 1][:, I // 2:], val_tab[2, 1][:].indirect(lists[1][:, 16:]))
-        for b in range(BOOKS):
-            turn(0, picked[0, b], False, b == 0, b == BOOKS - 1)
+        turn(0, add("pair0", picked[0, 0], picked[0, 1]), False, True, False)
+        turn(0, picked[0, 2], False, False, True)
         pair1 = add("pair1", picked[1, 0], picked[1, 1])
         turn(2, picked[2, 2], True, True, False)
         turn(1, add("triple1", pair1, picked[1, 2], "scale_tab2"), False, True, True)

from contextlib import ExitStack

import concourse.mybir as mybir
from concourse.masks import make_identity

D, I, Q, E, U = 512, 512, 256, 512, 512
FLOPS = 2 * (3 * D * Q * I + I * E * Q)

F32 = mybir.dt.float32
BF16 = mybir.dt.bfloat16
I32 = mybir.dt.int32
U32 = mybir.dt.uint32
U16 = mybir.dt.uint16
U8 = mybir.dt.uint8
FP8X4 = mybir.dt.float8_e4m3fn_x4
FP4X4 = mybir.dt.float4_e2m1fn_x4
ACT = mybir.ActivationFunctionType
ALU = mybir.AluOpType
AXIS = mybir.AxisListType

P = 128
PACK = 4
BOOKS = 3
WIN = 704
WIN16 = 1024
WIN_SCALAR = U + 8
HALVES = Q // P
ON_VECTOR = ((2, 2), (3, 2))


def tile_attend_additivekeys_pl_kernel(tc, query, ba_words, ba_scales, bb_words, bb_scales, bc_words, bc_scales,
                                        size, ca, cb, cc, vsc, offs, offs2, offs3, out_0, out_1, out_2):
    nc = tc.nc
    with ExitStack() as ctx:
        keep = ctx.enter_context(tc.tile_pool(name="keep", bufs=1))
        psum = ctx.enter_context(tc.psum_pool(name="psum", bufs=1))

        places = [(j, b) for j in range(PACK) for b in range(BOOKS)]
        lists = [keep.tile([P, I // 16], U16, name=f"list{b}") for b in range(BOOKS)]
        key_tab = [keep.tile([P, 2 * WIN16], U8, name="key_tab0"),
                   keep.tile([P, WIN], I32, name="key_tab1"),
                   keep.tile([P, WIN], I32, name="key_tab2")]
        scale_tab = [keep.tile([P, WIN], U8, name=f"scale_tab{b}", tag=f"scale_tab{b}", align_bytes=64) for b in range(BOOKS)]
        val_tab = {(j, b): keep.tile([P, WIN if (j, b) in ON_VECTOR else WIN_SCALAR], F32, name=f"val_tab{j}{b}",
                                     tag=f"val_tab{j}{b}")
                   for j, b in places}
        ident = keep.tile([P, P], F32, name="ident")

        warm = keep.tile([P, 2], F32, name="warm")
        nc.gpsimd.memset(warm[:, :1], 0.0)
        nc.scalar.activation(warm[:, 1:], warm[:, :1], ACT.Exp)
        for b in range(BOOKS):
            nc.vector.memset(scale_tab[b][:].bitcast(I32), 0)
        nc.vector.memset(key_tab[0][:, 2 * U:].bitcast(I32), 0)
        for b in (1, 2):
            nc.vector.memset(key_tab[b][:, U:], 0)
        nc.gpsimd.memset(val_tab[places[0]][:, U:], 0.0)
        make_identity(nc, ident[:])
        size_t = keep.tile([P, PACK], F32, name="size_t")
        nc.gpsimd.dma_start(size_t[:], size.rearrange("o (p t) -> (o p) t", t=PACK))
        for place in places[1:]:
            nc.gpsimd.memset(val_tab[place][:, U:], 0.0)

        q_raw = keep.tile([P, PACK, Q], F32, name="q_raw")
        vsc_t = keep.tile([P, PACK], F32, name="vsc_t", tag="vsc", align_bytes=64)
        val_rows = [table.rearrange("(p t) u -> p (t u)", t=PACK) for table in (ca, cb, cc)]

        def load_values(j, b):
            nc.sync.dma_start(val_tab[j, b][:, :U], val_rows[b][:, U * j:U * (j + 1)])

        def load_keys(b, words):
            nc.sync.dma_start(key_tab[b][:, :U], words[0].rearrange("p n t -> p (n t)").bitcast(I32))

        def load_scale_rows(b, scales, quads):
            for quad in quads:
                nc.sync.dma_start(scale_tab[b][32 * quad:32 * quad + 4, :U].bitcast(I32),
                                  scales[0, 4 * quad:4 * quad + 4, :].bitcast(I32))

        nc.sync.dma_start(key_tab[0][:, :2 * U].bitcast(I32), ba_words[0].bitcast(I32))
        nc.sync.dma_start(lists[0][:], offs)
        load_values(0, 0)
        nc.sync.dma_start(lists[1][:], offs2)
        load_keys(1, bb_words)
        load_scale_rows(0, ba_scales, (0,))
        load_values(0, 1)
        load_scale_rows(0, ba_scales, (1,))
        load_keys(2, bc_words)
        nc.sync.dma_start(lists[2][:], offs3)
        load_values(0, 2)
        load_scale_rows(0, ba_scales, (2, 3))
        nc.sync.dma_start(q_raw[:], query.rearrange("(p t) q -> p t q", t=PACK))
        load_scale_rows(1, bb_scales, (0,))
        load_values(1, 0)
        load_scale_rows(1, bb_scales, (1, 2, 3))
        for place in ((1, 1), (1, 2), (2, 0)):
            load_values(*place)
        load_scale_rows(2, bc_scales, range(4))
        for place in ((2, 2), (2, 1), (3, 2)):
            load_values(*place)
        nc.sync.dma_start(vsc_t[:], vsc.rearrange("(p t) o -> p (t o)", t=PACK))
        load_values(3, 0)
        load_values(3, 1)

        key = [keep.tile([P, 2 * I], U8, name="key0", align_bytes=64),
               keep.tile([P, I], U32, name="key1", align_bytes=64),
               keep.tile([P, I], U32, name="key2", align_bytes=64)]
        key_scale = [keep.tile([P, I], U8, name=f"key_scale{b}", align_bytes=64) for b in range(BOOKS)]
        nc.vector.tensor_copy(key[0][:].bitcast(U16), key_tab[0][:].bitcast(U16).indirect(lists[0][:]))
        for b in (1, 2):
            nc.vector.tensor_copy(key[b][:], key_tab[b][:].bitcast(U32).indirect(lists[b][:]))
        q_bf = keep.tile([P, Q, PACK], BF16, name="q_bf", align_bytes=64)
        nc.vector.tensor_copy(q_bf[:].rearrange("p (c i) t -> p c t i", i=4),
                              q_raw[:].rearrange("p t (c i) -> p c t i", i=4))
        q_codes = keep.tile([P, Q], U32, name="q_codes", align_bytes=64)
        q_scales = keep.tile([P, Q], U8, name="q_scales", align_bytes=64)
        score = [psum.tile([P, I], F32, name=f"score{h}", tag=f"score{h}") for h in range(HALVES)]
        for b in range(BOOKS):
            nc.vector.tensor_copy(key_scale[b][:], scale_tab[b][:].indirect(lists[b][:]))
            if b == 0:
                nc.vector.quantize_mx(out=q_codes[:].bitcast(FP8X4), scales=q_scales[:],
                                      in_=q_bf[:].rearrange("p q t -> p (q t)"))
            for h in range(HALVES):
                cols = slice(P * h, P * (h + 1))
                nc.tensor.matmul_mx(out=score[h][:], lhsT=q_codes[:, cols].bitcast(FP8X4), lhsT_scale=q_scales[:, cols],
                                    rhs=key[b][:].bitcast(FP4X4 if b == 0 else FP8X4), rhs_scale=key_scale[b][:],
                                    start=(b == 0), stop=(b == BOOKS - 1))

        summed = [psum.tile([P, PACK, P], F32, name=f"summed{j}", tag=f"sum{j}") for j in range(PACK)]

        picked = {}

        def gather(j, b, tag=None):
            picked[j, b] = keep.tile([P, I], F32, name=f"picked{j}{b}", tag=tag or f"picked{j}{b}")
            if (j, b) in ON_VECTOR:
                nc.vector.tensor_copy(picked[j, b][:].bitcast(U32).rearrange("p (t s) -> p s t", t=PACK),
                                      val_tab[j, b][:].bitcast(U32).indirect(lists[b][:]))
            else:
                nc.scalar.activation(picked[j, b][:], val_tab[j, b][:].indirect(lists[b][:]), ACT.Copy)

        def add(name, left, right, tag=None):
            both = keep.tile([P, I], F32, name=name, tag=tag or name, align_bytes=64)
            nc.gpsimd.tensor_tensor(both[:], left[:], right[:], ALU.add)
            return both

        def turn(j, tile, dealt, opens, closes):
            for t in range(PACK):
                plane = tile[:, P * t:P * (t + 1)] if dealt else tile[:, t:I:PACK]
                nc.tensor.matmul(summed[j][:, t, :], lhsT=plane, rhs=ident[:], is_transpose=True,
                                 start=(opens and t == 0), stop=(closes and t == PACK - 1))

        def scale_values(j, v_bf):
            nc.vector.tensor_tensor(v_bf, summed[j][:].rearrange("p t m -> p m t"),
                                    vsc_t[:].unsqueeze(1).to_broadcast([P, P, PACK]), ALU.mult)

        for place in places[:7] + places[8:9]:
            gather(*place)
        picked[2, 1] = keep.tile([P, I], F32, name="picked21")
        nc.scalar.activation(picked[2, 1][:, :I // 2], val_tab[2, 1][:].indirect(lists[1][:, :16]), ACT.Copy)
        nc.vector.tensor_copy(picked[2, 1][:, I // 2:], val_tab[2, 1][:].indirect(lists[1][:, 16:]))
        turn(0, add("pair0", picked[0, 0], picked[0, 1]), False, True, False)
        turn(0, picked[0, 2], False, False, True)
        pair1 = add("pair1", picked[1, 0], picked[1, 1])
        turn(2, picked[2, 2], True, True, False)
        turn(1, add("triple1", pair1, picked[1, 2], "scale_tab2"), False, True, True)
        turn(2, add("pair2", picked[2, 0], picked[2, 1]), False, False, True)

        size_row = psum.tile([P, PACK, P], F32, name="size_row", tag="size")
        for t in range(PACK):
            nc.tensor.transpose(size_row[:, t, :], size_t[:, t:t + 1].to_broadcast([P, P]), ident[:])
        neg_max = keep.tile([P, HALVES], F32, name="neg_max")
        row_sum = keep.tile([P, HALVES], F32, name="row_sum", tag="row_sum", align_bytes=64)
        inv_sum = keep.tile([P, HALVES], F32, name="inv_sum", tag="inv_sum", align_bytes=64)
        shared = keep.tile([P, I + I // 2], F32, name="shared")
        prob = [keep.tile([P, I], F32, name="prob0")[:], shared[:, I // 2:]]
        for h in range(HALVES):
            nc.vector.tensor_reduce(neg_max[:, h:h + 1], score[h][:], AXIS.X, ALU.max, negate=True)
            nc.scalar.activation(prob[h], score[h][:], ACT.Exp,
                                 bias=neg_max[:, h:h + 1], accum_out=row_sum[:, h:h + 1])
        gather(3, 2)
        turn(3, picked[3, 2], True, True, False)
        nc.vector.reciprocal(inv_sum[:], row_sum[:])
        w_woven = keep.tile([P, Q, PACK], BF16, name="w_woven", align_bytes=64)
        v_woven = keep.tile([P, 2 * P, PACK], BF16, name="v_woven", tag="row_sum", align_bytes=64)
        w_turned = psum.tile([P, HALVES, 2, P], F32, name="w_turned", tag="w")
        for h in range(HALVES):
            w_bf = keep.tile([P, I], BF16, name=f"w_bf{h}")
            nc.vector.scalar_tensor_tensor(w_bf[:].rearrange("p (s t) -> p s t", t=PACK),
                                           prob[h].rearrange("p (s t) -> p s t", t=PACK), inv_sum[:, h:h + 1],
                                           size_row[:].rearrange("p t s -> p s t"), ALU.mult, ALU.mult)
            for u in range(2):
                nc.tensor.transpose(w_turned[:, h, u, :], w_bf[:].bitcast(F32)[:, u:I // 2:2], ident[:])
        gather(3, 0)
        turn(3, picked[3, 0], False, False, False)
        for half in range(2):
            nc.scalar.activation(shared[:, I // 2 * half:I // 2 * (half + 1)],
                                 val_tab[3, 1][:].indirect(lists[1][:, 16 * half:16 * (half + 1)]), ACT.Copy)
        turn(3, shared, False, False, True)
        nc.scalar.copy(w_woven[:].rearrange("p q t -> p (q t)").bitcast(F32).rearrange("p (h q u) -> p h q u", h=HALVES, u=2),
                       w_turned[:].rearrange("p h u q -> p h q u"))
        for j in range(2):
            scale_values(j, v_woven[:, P * j:P * (j + 1), :])
        third_bf = keep.tile([P, P, PACK], BF16, name="third_bf", tag="inv_sum", align_bytes=64)
        scale_values(2, third_bf[:])

        early_codes = keep.tile([P, 2 * P], U32, name="early_codes", align_bytes=64)
        early_scales = keep.tile([P, 2 * P], U8, name="early_scales", align_bytes=64)
        w_codes = keep.tile([P, Q], U32, name="w_codes", align_bytes=64)
        w_scales = keep.tile([P, Q], U8, name="w_scales", align_bytes=64)
        acc_early = [psum.tile([P, 2, P], F32, name=f"acc_early{h}", tag=f"score{h}") for h in range(HALVES)]
        acc = [psum.tile([P, 2, P], F32, name=f"acc_late{h}", tag=("size", "w")[h]) for h in range(HALVES)]
        o_sb = keep.tile([P, PACK, Q], F32, name="o_sb")
        o_rows = out_0.rearrange("(p t) q -> p t q", t=PACK)
        o_bf = keep.tile([P, Q, PACK], BF16, name="o_bf", tag="vsc", align_bytes=64)

        def product(j, v_codes, v_scales):
            for h in range(HALVES):
                cols = slice(P * h, P * (h + 1))
                nc.tensor.matmul_mx(out=acc[h][:, j % 2, :], lhsT=v_codes.bitcast(FP8X4), lhsT_scale=v_scales,
                                    rhs=w_codes[:, cols].bitcast(FP8X4), rhs_scale=w_scales[:, cols],
                                    start=True, stop=True)

        def unload(h):
            copy = nc.vector.tensor_copy if h == 0 else nc.scalar.copy
            copy(o_sb[:, 2:, P * h:P * (h + 1)], acc[h][:])

        def weave(h):
            copy = nc.vector.tensor_copy if h == 0 else nc.scalar.copy
            copy(o_bf[:, P * h:P * (h + 1), 2:], acc[h][:].rearrange("p j q -> p q j"))

        def store(u):
            queue = nc.sync if u == 0 else nc.scalar
            queue.dma_start(o_rows[:, 2 * u:2 * u + 2, :], o_sb[:, 2 * u:2 * u + 2, :])

        nc.vector.quantize_mx(out=early_codes[:].bitcast(FP8X4), scales=early_scales[:],
                              in_=v_woven[:].rearrange("p m t -> p (m t)"))
        nc.vector.quantize_mx(out=w_codes[:].bitcast(FP8X4), scales=w_scales[:],
                              in_=w_woven[:].rearrange("p m t -> p (m t)"))
        for h in range(HALVES):
            rows = slice(P * h, P * (h + 1))
            for j in range(2):
                cols = slice(P * j, P * (j + 1))
                nc.tensor.matmul_mx(out=acc_early[h][:, j, :], lhsT=early_codes[:, cols].bitcast(FP8X4),
                                    lhsT_scale=early_scales[:, cols], rhs=w_codes[:, rows].bitcast(FP8X4),
                                    rhs_scale=w_scales[:, rows], start=True, stop=True)
            nc.scalar.copy(o_sb[:, :2, rows], acc_early[h][:])
        store(0)
        late_codes = [keep.tile([P, P], U32, name=f"late_codes{j}", align_bytes=64) for j in range(2)]
        late_scales = [keep.tile([P, P], U8, name=f"late_scales{j}", align_bytes=64) for j in range(2)]
        last_bf = keep.tile([P, P, PACK], BF16, name="last_bf", align_bytes=64)
        scale_values(3, last_bf[:])
        nc.vector.quantize_mx(out=late_codes[0][:].bitcast(FP8X4), scales=late_scales[0][:],
                              in_=third_bf[:].rearrange("p m t -> p (m t)"))
        product(2, late_codes[0][:], late_scales[0][:])
        nc.vector.quantize_mx(out=late_codes[1][:].bitcast(FP8X4), scales=late_scales[1][:],
                              in_=last_bf[:].rearrange("p m t -> p (m t)"))
        product(3, late_codes[1][:], late_scales[1][:])
        for h in range(HALVES):
            rows = slice(P * h, P * (h + 1))
            nc.vector.tensor_copy(o_bf[:, rows, :2], o_sb[:, :2, rows].rearrange("p j q -> p q j"))
        for h in range(HALVES):
            weave(h)
            unload(h)
        store(1)

        o_codes = keep.tile([P, Q], U32, name="o_codes", align_bytes=64)
        o_scales = keep.tile([P, Q], U8, name="o_scales", align_bytes=64)
        for h in range(HALVES):
            cols = slice(P * h, P * (h + 1))
            nc.vector.quantize_mx(out=o_codes[:, cols].bitcast(FP8X4), scales=o_scales[:, cols],
                                  in_=o_bf[:, cols, :].rearrange("p q t -> p (q t)"))
        nc.sync.dma_start(out_1[0].rearrange("p c t -> p (c t)").bitcast(I32), o_codes[:].bitcast(I32))
        for quad in range(4):
            queue = nc.sync if quad < 2 else nc.scalar
            queue.dma_start(out_2[0, 4 * quad:4 * quad + 4, :].bitcast(I32),
                            o_scales[32 * quad:32 * quad + 4, :].bitcast(I32))
